import numpy as np, ml_dtypes
CORES = [16,18,20,22]
N = 4
import mx_ref
BF = ml_dtypes.bfloat16
def gentries(a):
    return np.ascontiguousarray(a.reshape(8, 16, -1).transpose(0, 2, 1)).reshape(8, -1)
def gtable(e):
    e = np.asarray(e); return np.ascontiguousarray(e.reshape(8, -1, 16).transpose(0, 2, 1)).reshape(128, -1).astype(np.int32)
def gcols(t, e):
    v = np.concatenate([t.reshape(8, 16, -1, 4), np.zeros((8, 16, 1, 4), BF)], axis=2)
    return np.ascontiguousarray(np.stack([v[g][:, e[g]] for g in range(8)])).reshape(128, -1)
def tile(rs):
    return np.stack(rs, axis=2).reshape(128, -1).astype(BF)
def cut(t, i, w=512):
    return t[:, w * i:w * i + w]
def pick(q, e):
    c = np.concatenate([q[0].reshape(128, -1, 4), np.zeros((128, 1, 4), np.uint8)], axis=1); s = np.concatenate([q[1], np.ones((16, 1), np.uint8)], axis=1)
    return (np.ascontiguousarray(c[:, e].reshape(128, -1)), np.ascontiguousarray(s[:, e]))
def join(*qs):
    return (np.concatenate([q[0] for q in qs], axis=1), np.concatenate([q[1] for q in qs], axis=1))
def put(q, e, v):
    c, s = q[0].reshape(128, -1, 4).copy(), q[1].copy(); c[:, e] = v[0].reshape(128, -1, 4); s[:, e] = v[1]
    return (c.reshape(128, -1), s)
def pk(c, s):
    return (np.ascontiguousarray(c), mx_ref.live(s))
def emit(q):
    return q[0], q[1]
def packed(v, rng):
    q = [mx_ref.quantize(np.ascontiguousarray(v[r])) for r in range(N)]
    return np.stack([a for a, b in q]), np.stack([mx_ref.plane(b, rng) for a, b in q])
def values_of_codes():
    e, c = np.zeros((128, 128, 4), np.float32), np.zeros((128, 2, 4), np.uint8)
    e[np.arange(128), np.arange(128), 0] = 1
    c[:127, :, 0] = np.arange(256).reshape(2, 128).T[:127]
    return mx_ref.matmul(mx_ref.quantize(e.reshape(128, 512).astype(BF)), (c.reshape(128, 8), np.full((16, 2), 127, np.uint8))).T.reshape(-1).astype(np.float64)
CODE_VALUE, SCALE_VALUE = values_of_codes(), 2.0 ** (np.arange(256) - 127.0)
def decode(q):
    return (CODE_VALUE[q[0]].reshape(16, 8, -1, 4) * SCALE_VALUE[q[1]][:, None, :, None] + 0.0).reshape(128, -1).astype(np.float32)
def f(rng, *shape):
    return mx_ref.flush((rng.standard_normal(shape, dtype=np.float32) * np.exp2(rng.integers(-2, 3, shape[:-1] + (1,)))).astype(BF))
def wide(rng, *shape, cols=0):
    v = rng.standard_normal(shape, dtype=np.float32) * np.exp2(rng.integers(-12, 13, shape)).astype(np.float32)
    if cols: v *= np.repeat(np.exp2(rng.integers(-cols, cols + 1, shape[:-2] + (1, shape[-1] // 4))) * (rng.random(shape[:-2] + (1, shape[-1] // 4)) > 0.0625), 4, axis=-1).astype(np.float32)
    return mx_ref.flush(v.astype(BF))
C, L, R = 384, 320, 3
def read(pool, at, up):
    a = gcols(pool, at).astype(np.float32)
    b = gcols(pool, np.take_along_axis(up, at, axis=1)).astype(np.float32)
    return mx_ref.quantize(np.ascontiguousarray((a + b).astype(BF)))
def big(v):
    v = v.astype(np.float32)
    v[np.abs(v) < np.float32(2.0 ** -16)] = 0
    return v.astype(BF)
def numbers_of(rng):
    return {"x": big(f(rng, N, 128, 4 * C)), "u": np.array(f(rng, N, 128, 512))}
def listed(p, t):
    return {"par": np.stack([gtable(a) for a in p]), "top": np.stack([gtable(a) for a in t])}
def parents(rng):
    return np.where(rng.random((N, 8, C)) < 0.125, np.arange(C), rng.integers(0, C, (N, 8, C)))
def tops(rng):
    return rng.integers(0, C, (N, 8, L))
def among(rng, k, h):
    o = np.argsort(k, kind="stable")
    return o[rng.integers(np.searchsorted(k[o], h), np.searchsorted(k[o], h, side="right"))]
def weights(rng, w):
    c, p = packed(w, rng)
    return {"wc": c, "ws": p}
def still(rng, k):
    w = np.zeros((N, 128, 4, 128, 4), np.float32)
    i = np.arange(128)
    for b in range(4): w[:, i, b, i, b] = k
    return weights(rng, w.reshape(N, 128, 2048).astype(BF))
def signs(rng):
    return np.stack([rng.permutation(8) % 2 * 2.0 - 1.0 for r in range(N)])
def setup_inputs(rng):
    return {**numbers_of(rng), **listed(parents(rng), tops(rng)), **weights(rng, f(rng, N, 128, 2048))}
def setup_inputs_ties(rng):
    d = numbers_of(rng)
    e = rng.permutation(N)
    x = d["x"].reshape(N, 8, 16, C, 4)
    p, q = parents(rng), tops(rng)
    for r in range(N):
        k, h = (np.zeros(C, int), np.zeros(L, int)) if r == e[0] else (rng.permutation(C) % 3, rng.permutation(L) % 3)
        a = x[r][:, :8, :3].copy()
        a[:, :, 2] = 0
        x[r][:, :8] = a[:, :, k]
        p[r] = among(rng, k, np.tile(k, (8, 1)))
        q[r] = among(rng, k, np.tile(h, (8, 1)))
    x[e[1]] = 0
    u = d["u"].reshape(N, 8, 16, 128, 4)
    u[:, :, 8:, ::16] = 0
    w = np.array(f(rng, N, 128, 2048)).reshape(N, 8, 16, 4, 8, 16, 4)
    w[:, :, :, :, :, :8] = 0
    return {"x": x.reshape(N, 128, 4 * C), "u": u.reshape(N, 128, 512), **listed(p, q), **weights(rng, w.reshape(N, 128, 2048))}
def setup_inputs_near(rng):
    d = numbers_of(rng)
    x = d["x"].astype(np.float32).reshape(N, 8, 16, C, 4)
    m = np.arange(C) // 2
    g = ((m[:, None] >> np.arange(8)) & 1) * np.exp2(np.arange(8) - 23.0)
    a = np.repeat(rng.choice([-0.5, 0.5], (N, 8, C // 2)), 2, axis=-1)
    s = np.repeat(rng.choice([-1.0, 1.0], (N, 8, C // 2)), 2, axis=-1)
    x[:, :, 0] = 0
    x[:, :, 0, :, 0] = a
    x[:, :, 8] = g[:, :4] * s[..., None]
    x[:, :, 9] = g[:, 4:] * s[..., None]
    x[:, :, 10:] = rng.integers(4, 8, (N, 8, 6, C, 4)) * rng.choice([-1.0, 1.0], (N, 8, 6, C, 4)) * 2.0 ** -20
    u = d["u"].reshape(N, 128, 128, 4)
    one = rng.permutation(N) % 2 == 0
    x *= np.where(one, 1.0, 2.0 ** -6).astype(np.float32)[:, None, None, None, None]
    k = np.where(one, 1.0, 2.0 ** -30).astype(np.float32).astype(BF)
    u[:, :, ::16] = 0
    for h in range(0, 128, 16):
        u[:, h, h, 0] = k
        u[:, h + 8:h + 10, h] = k[:, None, None]
    p = np.repeat(rng.integers(0, C, (N, 8, C // 2)), 2, axis=-1)
    q = rng.permuted(np.tile(np.arange(C), (N, 8, 1)), axis=-1)[:, :, :L]
    return {"x": x.reshape(N, 128, 4 * C).astype(BF), "u": u.reshape(N, 128, 512), **listed(p, q), **still(rng, 64)}
def setup_inputs_huge(rng):
    d = numbers_of(rng)
    x = 2.0 ** 28 * (1.25 + 0.5 * rng.random((N, 128, C, 4)))
    one = rng.permutation(N) < N // 2
    p, q = parents(rng), tops(rng)
    for r in range(N):
        k, h = (np.zeros(C, int), np.zeros(L, int)) if one[r] else (rng.permutation(C) % 2, rng.permutation(L) % 2)
        x[r] *= (1.0 - 2.0 * k)[None, :, None]
        p[r] = among(rng, k, np.tile(k, (8, 1)))
        q[r] = among(rng, k, np.tile(h, (8, 1)))
    u = d["u"].reshape(N, 128, 128, 4)
    a = 2.0 ** 30 * (1 - 0.25 * rng.random((N, 128, 8, 4))) * signs(rng)[:, None, :, None]
    u[:, :, ::16] = a.astype(np.float32).astype(BF)
    return {"x": x.astype(np.float32).reshape(N, 128, 4 * C).astype(BF), "u": u.reshape(N, 128, 512), **listed(p, q), **still(rng, 16)}
def setup_inputs_forest(rng):
    d = setup_inputs(rng)
    p, q = parents(rng), tops(rng)
    e = rng.permutation(N)
    p[e[0]] = np.arange(C)
    p[e[1]] = rng.integers(0, C, (8, 1))
    p[e[2]] = (np.arange(C) + 1) % C
    q[e[3]] = rng.integers(0, C, (8, 1))
    return {**d, **listed(p, q)}
def setup_inputs_spread(rng):
    d = setup_inputs(rng)
    d["x"] = big(wide(rng, N, 128, 4 * C, cols=6))
    return d
def check_inputs(d):
    b = []
    for k in ("x", "u"):
        a = np.abs(d[k].astype(np.float32))
        if not (np.isfinite(a).all() and ((a == 0) | (a >= 2.0 ** -30) & (a <= 2.0 ** 30)).all()): b.append("a value of " + k)
    for k in ("par", "top"):
        if not ((d[k] >= 0) & (d[k] < C)).all(): b.append("an entry of " + k)
    return b
def reference(x, u, par, top, wc, ws):
    qu = [mx_ref.quantize(u[r]) for r in range(N)]
    lay = [pk(wc[r], ws[r]) for r in range(N)]
    pool = [x[r] for r in range(N)]
    up = [gentries(par[r]) for r in range(N)]
    at = [gentries(top[r]) for r in range(N)]
    for t in range(R):
        score, sent = [], []
        for r in range(N):
            q = read(pool[r], at[r], up[r])
            score.append(mx_ref.matmul(qu[r], q)[::16] + np.float32(0.0))
            sent.append(mx_ref.quantize(tile([np.maximum(mx_ref.matmul(pick(lay[r], np.arange(128 * b, 128 * b + 128)), q), np.float32(0.0)) * np.float32(0.015625) for b in range(4)])))
        came = decode(join(*sent)).astype(BF)
        for r in range(N):
            n = np.where(score[r] >= 0, C + L * t + np.arange(L), np.take_along_axis(up[r], at[r], axis=1))
            o = np.argsort(-score[r], axis=1, kind="stable")
            pool[r] = np.concatenate([pool[r], cut(came, (r - 1) % N, 4 * L)], axis=1)
            up[r] = np.concatenate([up[r], at[r]], axis=1)
            at[r] = np.take_along_axis(n, o, axis=1)
    y, ol = np.zeros((N, 128, L), np.float32), np.zeros((N, 8, L), np.float32)
    oc, osc = np.zeros((N, 128, 4 * L), np.uint8), np.zeros((N, 16, L), np.uint8)
    for r in range(N):
        q = read(pool[r], at[r], up[r])
        y[r] = mx_ref.matmul(qu[r], q)
        ol[r] = at[r]
        oc[r], osc[r] = emit(q)
    return {"y": y, "ol": ol, "oc": oc, "osc": osc}

@@ -1,0 +1,394 @@
+from concourse.mybir import dt, AluOpType, ActivationFunctionType
+
+C, L, R = 384, 320, 3
+NODES = C + L * R
+HELD = C + L * (R - 1)
+K = L // 16
+DSS = (7, 8, 8)
+LATE = (4, 0, 0)
+DS, DV = max(DSS), K - min(DSS)
+SEG = L + 8
+BIG = 1.0e28
+HOLD = 2048.0
+BANK = 512
+CODES = "float8_e4m3fn_x4"
+
+WIDTHS = {
+    "bfloat16": {"xs": 4 * C, "us": 512, "ones": 520, "eb": 520, "rz": L, "pool": 4 * HELD, "vt": 4 * NODES, "at": 4 * L,
+                 "z": 4 * L, "h": 4 * L, "ne": L, "nc": L, "fl": DV * L, "fs": DV * (L // 2), "sg": DS * SEG, "sj": DS * SEG},
+    "float32": {"mk": L, "ar": L, "ax": L, "cols": 8, "newc": R * K, "x15": K, "pt": 2 * NODES + L, "bm": L, "ff": L,
+                "t1": K, "t2": K, "t3": K, "nrow": L, "acc": 2 * K, "c1": K, "xx": L, "ys": L},
+    "int32": {"pari": C // 16, "topi": K, "ui": 8, "di": L, "dm": L, "ni": R * K},
+    "uint16": {"uo": 8, "paru": C // 16, "par4": 4 * (C // 16), "topu": (R + 1) * K, "idx": K, "rv": K, "rs": K},
+    CODES: {"wq": 512, "uq": 128, "urq": 128, "eq": 512, "zq": L},
+    "uint8": {"wp": 512, "up": 128, "urp": 128, "ep": 512, "zp": L},
+}
+SCRATCH = {_n: ("sbuf", [128, _w], _d) for _d in WIDTHS for _n, _w in WIDTHS[_d].items()}
+SCRATCH["ps"] = ("psum", [128, 8 * BANK], "float32")
+for _t in range(R):
+    SCRATCH["hq%d" % _t] = ("sbuf", [128, L], CODES)
+    SCRATCH["hp%d" % _t] = ("sbuf", [128, L], "uint8")
+    SCRATCH["lq%d" % _t] = ("sbuf", [128, L], CODES)
+    SCRATCH["lp%d" % _t] = ("sbuf", [128, L], "uint8")
+
+SEMAPHORES = ["cv", "cs", "ct", "cg", "dx", "du", "dpar", "dtop", "dwc", "dws", "dout", "sent"] + ["arr%d" % _t for _t in range(R)]
+
+
+def rank_program(g, core, T, topo):
+    rank = T.rank_of(core)
+    if rank is None:
+        return
+    nxt = T.cores[(rank + 1) % len(T.cores)]
+    rid, pid = topo.addr(nxt)[0], topo.addr(nxt)[1]
+    wide = topo.mask(core, nxt)
+    lanes = len(topo.engines(core, nxt))
+    A, F = AluOpType, ActivationFunctionType
+
+    queue = {"v": g.vector, "s": g.scalar, "t": g.tensor, "g": g, "y": g.sync}
+    counter = {"v": "cv", "s": "cs", "t": "ct", "g": "cg"}
+    total = {}
+    known = {q: {} for q in queue}
+    clock = {}
+    wrote, read, banks = {}, {}, {}
+
+    def span(r):
+        return range(r[1], r[2], r[3] if len(r) > 3 else 1)
+
+    def ap(r):
+        if len(r) > 3:
+            return T[r[0]][:, r[1]:r[2]:r[3]]
+        return T[r[0]][:, r[1]:r[2]]
+
+    def wait(q, need):
+        for sem in sorted(need, key=lambda s: -need[s]):
+            val = need[sem]
+            if known[q].get(sem, 0) >= val:
+                continue
+            queue[q].wait_ge(T.sem[sem], val)
+            for s, v in clock[(sem, val)].items():
+                if known[q].get(s, 0) < v:
+                    known[q][s] = v
+
+    def issue(q, call, outs, ins, sem=None, step=1):
+        need = {}
+
+        def after(mark):
+            if mark is not None and need.get(mark[0], 0) < mark[1]:
+                need[mark[0]] = mark[1]
+
+        for r in list(ins) + list(outs):
+            if r[0] == "ps":
+                for oq, mark in banks.get(r[1] // BANK, {}).items():
+                    if oq != q:
+                        after(mark)
+        for r in ins:
+            if r[0] != "ps":
+                w = wrote.get(r[0], {})
+                for c in span(r):
+                    after(w.get(c))
+        for r in outs:
+            if r[0] != "ps":
+                w, rd = wrote.get(r[0], {}), read.get(r[0], {})
+                for c in span(r):
+                    after(w.get(c))
+                    for mark in rd.get(c, {}).items():
+                        after(mark)
+        for sa in list(need):
+            for sb in list(need):
+                if sa != sb and sa in need and sb in need and clock[(sb, need[sb])].get(sa, 0) >= need[sa]:
+                    del need[sa]
+        wait(q, need)
+        sem = sem or counter[q]
+        total[sem] = total.get(sem, 0) + step
+        mark = (sem, total[sem])
+        ck = dict(clock.get((sem, total[sem] - step), {}))
+        for s, v in known[q].items():
+            if ck.get(s, 0) < v:
+                ck[s] = v
+        ck[sem] = total[sem]
+        clock[mark] = ck
+        call().then_inc(T.sem[sem], step)
+        for r in list(ins) + list(outs):
+            if r[0] == "ps":
+                banks.setdefault(r[1] // BANK, {})[q] = mark
+        for r in ins:
+            if r[0] != "ps":
+                rd = read.setdefault(r[0], {})
+                for c in span(r):
+                    rd.setdefault(c, {})[sem] = total[sem]
+        for r in outs:
+            if r[0] != "ps":
+                w, rd = wrote.setdefault(r[0], {}), read.setdefault(r[0], {})
+                for c in span(r):
+                    w[c] = mark
+                    rd.pop(c, None)
+
+    def val(x):
+        return ap(x) if isinstance(x, tuple) else x
+
+    def refs(*xs):
+        return [x for x in xs if isinstance(x, tuple)]
+
+    def u8(r):
+        return ap(r).bitcast(dt.uint8)
+
+    def memset(out, c):
+        issue("v", lambda: g.vector.memset(ap(out), c), [out], [])
+
+    def ts(out, in0, s1, op0, s2=None, op1=None):
+        if op1 is None:
+            issue("v", lambda: g.vector.tensor_scalar(ap(out), ap(in0), val(s1), None, op0), [out], refs(in0, s1))
+        else:
+            issue("v", lambda: g.vector.tensor_scalar(ap(out), ap(in0), val(s1), val(s2), op0, op1), [out], refs(in0, s1, s2))
+
+    def tt(out, in0, in1, op, off=None):
+        if off is None:
+            issue("v", lambda: g.vector.tensor_tensor(ap(out), ap(in0), ap(in1), op), [out], [in0, in1])
+        else:
+            issue("v", lambda: g.vector.tensor_tensor(ap(out), ap(in0).indirect(ap(off)), ap(in1), op), [out], [in0, in1, off])
+
+    def copy(out, in_):
+        issue("v", lambda: g.vector.tensor_copy(ap(out), ap(in_)), [out], [in_])
+
+    def scan(out, d0, d1, init, op0, op1):
+        issue("v", lambda: g.vector.tensor_tensor_scan(ap(out), ap(d0), ap(d1), val(init), op0, op1), [out], refs(d0, d1, init))
+
+    def pick(q, out, win, off):
+        if q == "v":
+            issue("v", lambda: g.vector.tensor_copy(ap(out), ap(win).indirect(ap(off))), [out], [win, off])
+        else:
+            issue("s", lambda: g.scalar.activation(ap(out), ap(win).indirect(ap(off)), F.Copy), [out], [win, off])
+
+    def scatter(win, off, in_):
+        issue("v", lambda: g.vector.tensor_copy(ap(win).indirect(ap(off)), ap(in_)), [win], [off, in_])
+
+    def act(out, in_, func, bias=None, scale=None, accum=None):
+        kw = {}
+        if scale is not None:
+            kw["scale"] = scale
+        if bias is not None:
+            kw["bias"] = ap(bias)
+        if accum is not None:
+            kw["accum_out"] = ap(accum)
+        issue("s", lambda: g.scalar.activation(ap(out), ap(in_), func, **kw), refs(out, accum), refs(in_, bias))
+
+    def quant(q, p, in_):
+        issue("v", lambda: g.vector.quantize_mx(ap(q), ap(p), ap(in_)), [q, p], [in_])
+
+    def bank(b):
+        return ("ps", b * BANK, b * BANK + L)
+
+    def mm(b, w, x):
+        issue("t", lambda: g.tensor.matmul_mx(ap(bank(b)), ap(w[0]), ap(w[1]), ap(x[0]), ap(x[1]), True, True), [bank(b)], list(w) + list(x))
+
+    def iota(out, pattern, base, cm, loose=False):
+        if loose:
+            issue("g", lambda: g.iota(ap(out), pattern, base, cm, allow_small_or_imprecise_dtypes=True), [out], [])
+        else:
+            issue("g", lambda: g.iota(ap(out), pattern, base, cm), [out], [])
+
+    def load(q, sem, out, dst, src, behind=()):
+        issue(q, lambda: queue[q].dma_start(dst, src), [out], list(behind), sem, 16)
+
+    def store(q, dst, src, in_):
+        issue(q, lambda: queue[q].dma_start(dst, src), [], [in_], "dout", 16)
+
+    def whole(name):
+        return (name, 0, SCRATCH[name][1][1])
+
+    def plane(name, t, a, b):
+        w = SCRATCH[name][1][1] // 4
+        return (name, t * w + a, t * w + b)
+
+    def side(q, p, b):
+        return (q, 128 * b, 128 * b + 128), (p, 128 * b, 128 * b + 128)
+
+    PC = C // 16
+    col_c, col_a = ("cols", 0, 1), ("cols", 1, 2)
+    qz, qu, qur = (whole("zq"), whole("zp")), (whole("uq"), whole("up")), (whole("urq"), whole("urp"))
+    SV, SS, LAY, DEC = 0, 1, (2, 3), (4, 5, 6, 7)
+
+    load("y", "dx", whole("xs"), T.xs[:], T.x[:])
+    load("s", "dpar", whole("pari"), T.pari[:], T.par[:])
+    load("s", "dtop", whole("topi"), T.topi[:], T.top[:])
+    load("y", "du", whole("us"), T.us[:], T.u[:])
+    load("y", "dwc", whole("wq"), u8(whole("wq")), T.wc[:], [("xs", 0, 1)])
+    load("y", "dws", whole("wp"), T.wp[:], T.ws[:])
+
+    iota(whole("di"), [[0, K], [-1, 16]], 16, 1)
+    iota(("pt", 0, C), [[1, C]], 0, 0, True)
+    iota(whole("ui"), [[16, 8]], 0, 0)
+    iota(whole("ni"), [[-L, R], [16, K]], -L, 0)
+    memset(whole("ones"), 1.0)
+    memset(whole("ar"), 9.0e29)
+    memset(whole("rz"), 1.0)
+    for k in range(DS):
+        memset(("sg", k * SEG + L, k * SEG + L + 1), -16.0 * k)
+    memset(("ar", 0, L, 16), -9.0e29)
+    memset(("rz", 0, L, 16), 0.0)
+    issue("g", lambda: g.affine_select(T.eb[:], T.ones[:], [[-1, 520]], A.is_equal, 0.0, 3, 4), [whole("eb")], [whole("ones")])
+    ts(whole("dm"), whole("di"), 15, A.bitwise_and)
+    ts(whole("mk"), whole("dm"), 0.5, A.subtract, -BIG, A.mult)
+    for t in range(4):
+        ts(("par4", t * PC, (t + 1) * PC), whole("pari"), 4.0, A.mult, float(t), A.add)
+    copy(whole("paru"), whole("pari"))
+    copy(("topu", 0, K), whole("topi"))
+    pick("s", ("pt", NODES, NODES + C), ("pt", 0, C), whole("paru"))
+    pick("s", ("pt", NODES + C, NODES + C + L), ("pt", 0, C), ("topu", 0, K))
+    ts(col_c, ("dm", 0, 1), 15.0, A.subtract, -HOLD, A.mult)
+    ts(col_a, ("dm", 0, 1), 1.0 - HOLD, A.mult, 15.0 * HOLD, A.add)
+    copy(whole("uo"), whole("ui"))
+    ts(whole("ax"), whole("mk"), -1.0, A.mult, HOLD, A.min)
+    ts(whole("newc"), whole("ni"), col_a, A.add)
+    ts(whole("x15"), whole("topi"), col_c, A.add)
+    for b in range(4):
+        quant(side("eq", "ep", b)[0], side("eq", "ep", b)[1], ("eb", 3 - b, 515 - b))
+
+    def first_top(t):
+        pick("s", plane("at", t, 0, L), plane("pool", t, 0, C), ("topu", 0, K))
+
+    copy(plane("pool", 0, 0, C), ("xs", 0, 4 * C, 4))
+    act(plane("pool", 1, 0, C), ("xs", 1, 4 * C, 4), F.Copy)
+    for t in (2, 3):
+        issue("g", lambda: g.affine_select(ap(plane("pool", t, 0, C)), ap(("xs", t, 4 * C, 4)), [[0, C]], A.is_ge, 0.0, 0, 0),
+              [plane("pool", t, 0, C)], [("xs", t, 4 * C, 4)])
+    iota(("pt", NODES - L, NODES), [[1, L]], C, 0, True)
+    first_top(0)
+    for t in range(4):
+        tt(plane("vt", t, 0, C), whole("xs"), plane("pool", t, 0, C), A.add, ("par4", t * PC, (t + 1) * PC))
+        if t == 1:
+            quant(qu[0], qu[1], whole("us"))
+    for t in range(3):
+        pick("s", ("z", t, 4 * L, 4), plane("vt", t, 0, C), ("topu", 0, K))
+        if t == 1:
+            pick("s", qur[1], qu[1], whole("uo"))
+    pick("v", ("z", 3, 4 * L, 4), plane("vt", 3, 0, C), ("topu", 0, K))
+
+    for r in range(R):
+        have = C + L * r
+        ds = DSS[r]
+        tops = ("topu", r * K, (r + 1) * K)
+        held = whole("x15") if r == 0 else ("xx", 15, L, 16)
+        hq, hp, lq, lp = (whole(n % r) for n in ("hq%d", "hp%d", "lq%d", "lp%d"))
+        later = list(range(4)) if r > 0 else []
+
+        def old_top(q):
+            if later:
+                t = later.pop(0)
+                pick(q, plane("at", t, 0, L), plane("pool", t, 0, have), tops)
+
+        quant(qz[0], qz[1], whole("z"))
+        old_top("s")
+        old_top("v")
+        if r == 0:
+            first_top(1)
+            issue("v", lambda: g.vector.tensor_copy(T.urq[:].bitcast(dt.uint32), T.uq[:].bitcast(dt.uint32).indirect(T.uo[:])),
+                  [qur[0]], [qu[0], whole("uo")])
+        else:
+            mm(SV, qur, qz)
+        for b in range(4):
+            mm(LAY[b % 2], side("wq", "wp", b), qz)
+            if b == 0 and r == 0:
+                mm(SV, qur, qz)
+            if b == 1:
+                mm(SS, qur, qz)
+            act(("h", b, 4 * L, 4), bank(LAY[b % 2]), F.Relu, scale=0.015625)
+
+        tt(whole("bm"), bank(SV), whole("mk"), A.min)
+        scan(whole("ff"), whole("ar"), whole("bm"), 0.0, A.min, A.max)
+
+        def own(k):
+            return ("ff", 16 * k + 15, 16 * k + 16)
+
+        def compare(k):
+            j, cut = (k - ds) * L, 16 * k + 16
+            ts(("fl", j, j + cut), ("ps", SV * BANK, SV * BANK + cut), own(k), A.is_ge, 0.5, A.subtract)
+            if cut < L:
+                ts(("fl", j + cut, j + L), ("ps", SV * BANK + cut, SV * BANK + L), own(k), A.is_gt, 0.5, A.subtract)
+
+        def count(k):
+            j, o, m = (k - ds) * L, (k - ds) * (L // 2), L // 2
+            scan(("fs", o, o + m), ("fl", j, j + m), ("fl", j + m, j + L), ("nc", 16 * k + 15, 16 * k + 16), A.add, A.add)
+
+        def signs(k):
+            act(("sg", k * SEG, k * SEG + L), bank(SS), F.Sign, bias=own(k), scale=-1.0)
+
+        def sums(k):
+            j, cut = k * SEG, 16 * k + 16
+            act(("sj", j, j + cut), ("sg", j, j + cut), F.Relu, accum=("acc", k, k + 1))
+            act(("sj", j + cut, j + L + 2), ("sg", j + cut, j + L + 2), F.Relu, scale=-1.0, accum=("acc", K + k, K + k + 1))
+
+        ts(whole("t1"), ("ff", 15, L, 16), 0.0, A.is_ge, -BIG, A.mult)
+        tt(whole("ne"), bank(SV), whole("ff"), A.not_equal)
+        tt(whole("t2"), whole("t1"), held, A.add)
+        compare(ds)
+        quant(hq, hp, whole("h"))
+        wait("g", {"cv": total["cv"]})
+        g.remote_dma(u8(lq), u8(hq), T.sem["arr%d" % r], T.sem.sent, pid, rid, wide)
+        g.remote_dma(ap(lp), ap(hp), T.sem["arr%d" % r], T.sem.sent, pid, rid, wide)
+        mark = ("arr%d" % r, 2 * lanes)
+        clock[mark] = {mark[0]: mark[1]}
+        wrote[lq[0]] = {c: mark for c in span(lq)}
+        wrote[lp[0]] = {c: mark for c in span(lp)}
+        tt(whole("t3"), whole("t2"), ("newc", r * K, (r + 1) * K), A.max)
+        scan(whole("nc"), whole("rz"), whole("ne"), 0.0, A.mult, A.add)
+        ts(whole("idx"), whole("t3"), col_c, A.subtract, float(L * (r + 1)), A.add)
+        ts(("sg", L + 1, ds * SEG, SEG), ("nc", 15, 16 * ds, 16), -1.0, A.mult)
+        if r == 0:
+            iota(("pt", C, NODES - L), [[-L, R - 1], [1, L]], NODES - L, 0, True)
+
+        signs(0)
+        signs(1)
+        pick("s", whole("nrow"), ("pt", NODES - L * (r + 1), NODES + have), whole("idx"))
+        for k in range(ds):
+            if 1 < k + 1 < ds:
+                signs(k + 1)
+            sums(k)
+            old_top("s")
+            if r == 0 and k < 2:
+                first_top(2 + k)
+        for k in range(ds, K):
+            if k + 1 < K:
+                compare(k + 1)
+            count(k)
+
+        for b in range(4):
+            mm(DEC[b], side("eq", "ep", b), (lq, lp))
+        order = ("pt", NODES + have + L, NODES + have + 2 * L)
+        fresh = [0, 1, 2, 3]
+
+        def new_sum():
+            b = fresh.pop(0)
+            tt(plane("vt", b, have, have + L), bank(DEC[b]), plane("at", b, 0, L), A.add)
+
+        ts(("rv", 0, K - ds), ("fs", L // 2 - 1, (K - ds) * (L // 2), L // 2), L // 2 - 16.0, A.add)
+        scatter(order, ("rv", 0, K - ds), ("nrow", 16 * ds, L))
+        while len(fresh) > LATE[r]:
+            new_sum()
+        tt(("c1", 0, ds), ("acc", K, K + ds), ("acc", 0, ds), A.subtract)
+        copy(("rs", 0, ds), ("c1", 0, ds))
+        scatter(order, ("rs", 0, ds), ("nrow", 0, 16 * ds))
+        if r + 1 < R:
+            for b in range(4):
+                act(plane("pool", b, have, have + L), bank(DEC[b]), F.Copy)
+        scan(whole("xx"), whole("ax"), order, 0.0, A.add, A.max)
+        moved = ("topu", (r + 1) * K, (r + 2) * K)
+        ts(moved, ("xx", 15, L, 16), col_c, A.subtract)
+        while fresh:
+            new_sum()
+        if r + 1 == R:
+            store("y", T.ol[:], T.pt[0:128:16, order[1]:order[2]], order)
+        for t in range(4):
+            pick("s" if t < (3 if LATE[r] > 1 else 2) else "v", ("z", t, 4 * L, 4), plane("vt", t, 0, have + L), moved)
+
+    quant(qz[0], qz[1], whole("z"))
+    mm(SS, qu, qz)
+    store("y", T.oc[:], u8(qz[0]), qz[0])
+    copy(whole("ys"), bank(SS))
+    for k in range(4):
+        store("s", T.osc[4 * k:4 * k + 4, :], T.zp[32 * k:32 * k + 4, :], qz[1])
+    store("y", T.y[:], T.ys[:], whole("ys"))
+
+    g.wait_ge(T.sem.sent, 2 * lanes * R)
+    for sem in sorted(total):
+        g.wait_ge(T.sem[sem], total[sem])

@@ -4,21 +4,24 @@ C, L, R = 384, 320, 3
 NODES = C + L * R
 HELD = C + L * (R - 1)
 K = L // 16
-DSS = (7, 8, 8)
-LATE = (4, 0, 0)
+M = L // 2
+DSS = (7, 7, 7)
+ZH = (1, 2, 2, 2)
+ORDER = "lx ip one lt lp lu ii ce pm cum n0 cm eb mk ar ca iu qe2 rz in qe1 qe0 n1 pu cc qe3 pp tu p40 sk p42 uo ax nw x15 pl0 pl1 pl2 ls lw p41 p43 vt0 pt pl3 a01 vt1 z000 qu a02 vt2 vt3 z002.s z001 up.v z003 a00 uq qz00 a03 mv0 ml00 ml01 bm00 ml02 h00 bm01 ml03 ff00 ms0 h01 ff01 G0i h02 E0j ne0 h03 G0h S0g nc0 t10 E0h S0e qh0 S0d G0j C0h go0 S0f E0n t20 G0s S0b E0o t30 B0f E0q B0d S0c sn0 E0k ix0 B0b E0s A0g B0g E0l S0a G0r C0j G0n A0e G0k G0m A0d G0l G0o E0i A0b C0s E0p B0c A0c G0q C0l E0m A0f C0n E0r B0e B0a A0a E0t C0m nr0 G0p C0i C0k C0p C0t C0q C0o C0r c10 md00 rv0 rs0 md02 sv0 md01 md03 d02 d03 w00 d01 ss0 d00 w02 xx01 xx00 to01 to00 w03 z110 z100 w01 z112.s z102 z113 z111 z103 z101 qz11 a13 qz10 a10.v mv1 a11 ml11 ml10 bm11 ml12 bm10 a12 ml13 ff11 ms1 ff10 E1l h10 ne1 h12 t11 G1h E1h h13 G1q E1k h11 t21 G1i G1j S1c qh1 S1f G1k nc1 go1 S1g E1i G1s E1q S1b t31 S1d G1l C1i sn1 E1t S1a E1o A1f E1r S1e E1j B1b ix1 B1g G1n B1e G1o C1j A1g G1r G1p E1p nr1 G1m E1n A1e C1q C1l C1k B1c E1m B1a A1b C1p E1s B1d md11 A1d C1m C1o md13 C1s C1t A1c md12 C1h C1n md10 C1r B1f w13 A1a rv1 d12 c11 sv1 d10 d13 rs1 w11 ss1 d11 xx10 xx11 to10 w10 z201 to11 w12 z213.s z203 z210 z212 z211 z202 z200 qz21 a23 qz20 a20.v mv2 a21 ml22 ml21 bm21 ml23 bm20 a22 ml20 ff21 ms2 ff20 G2o ne2 h21 G2i h20 nc2 E2p h23 E2h h22 E2j G2h S2c t12 G2m qh2 S2e G2r S2d E2m go2 E2l S2a G2q E2s B2c S2b G2l G2n C2h S2g E2n G2p B2b E2k B2g G2j B2e t22 E2i S2f sn2 E2o A2d G2s C2j t32 A2a G2k E2q B2d B2a C2o A2g C2n C2i E2r A2b ix2 A2f E2t A2c C2q C2t md23 C2k A2e C2l md21 C2p C2s md20 B2f C2r C2m nr2 md22 w23 rv2 c12 w20 sv2 rs2 ss2 w22 xx21 xx20 to21 w21 z310 z313 z311 to20 z312 z301 z302 z300 z303 qz31 qz30 my1 my0 oc y1 os3 os2 y0.s ol os1.s oy1.y oy0.s os0"
 DS, DV = max(DSS), K - min(DSS)
 SEG = L + 8
-BIG = 1.0e28
+BIG = 2.0 ** 93
 HOLD = 2048.0
+DROP = 2.0 ** 22
 BANK = 512
 CODES = "float8_e4m3fn_x4"
 
 WIDTHS = {
     "bfloat16": {"xs": 4 * C, "us": 512, "ones": 520, "eb": 520, "rz": L, "pool": 4 * HELD, "vt": 4 * NODES, "at": 4 * L,
-                 "z": 4 * L, "h": 4 * L, "ne": L, "nc": L, "fl": DV * L, "fs": DV * (L // 2), "sg": DS * SEG, "sj": DS * SEG},
-    "float32": {"mk": L, "ar": L, "ax": L, "cols": 8, "newc": R * K, "x15": K, "pt": 2 * NODES + L, "bm": L, "ff": L,
+                 "z": 4 * L, "h": 4 * L, "ne": L, "nc": L, "fl": DV * L, "fs": DV * M, "sg": DS * SEG, "sj": DS * SEG},
+    "float32": {"ir": L, "mk": L, "ar": L, "ax": L, "cols": 8, "newc": R * K, "x15": K, "pt": 2 * NODES + L, "bm": L, "ff": L,
                 "t1": K, "t2": K, "t3": K, "nrow": L, "acc": 2 * K, "c1": K, "xx": L, "ys": L},
-    "int32": {"pari": C // 16, "topi": K, "ui": 8, "di": L, "dm": L, "ni": R * K},
+    "int32": {"pari": C // 16, "topi": K, "ui": 12, "pi": 2, "pm": 2, "ni": R * K},
     "uint16": {"uo": 8, "paru": C // 16, "par4": 4 * (C // 16), "topu": (R + 1) * K, "idx": K, "rv": K, "rs": K},
     CODES: {"wq": 512, "uq": 128, "urq": 128, "eq": 512, "zq": L},
     "uint8": {"wp": 512, "up": 128, "urp": 128, "ep": 512, "zp": L},
@@ -26,10 +29,8 @@ WIDTHS = {
 SCRATCH = {_n: ("sbuf", [128, _w], _d) for _d in WIDTHS for _n, _w in WIDTHS[_d].items()}
 SCRATCH["ps"] = ("psum", [128, 8 * BANK], "float32")
 for _t in range(R):
-    SCRATCH["hq%d" % _t] = ("sbuf", [128, L], CODES)
-    SCRATCH["hp%d" % _t] = ("sbuf", [128, L], "uint8")
-    SCRATCH["lq%d" % _t] = ("sbuf", [128, L], CODES)
-    SCRATCH["lp%d" % _t] = ("sbuf", [128, L], "uint8")
+    for _n, _d in (("hq", CODES), ("hp", "uint8"), ("lq", CODES), ("lp", "uint8")):
+        SCRATCH[_n + str(_t)] = ("sbuf", [128, L], _d)
 
 SEMAPHORES = ["cv", "cs", "ct", "cg", "dx", "du", "dpar", "dtop", "dwc", "dws", "dout", "sent"] + ["arr%d" % _t for _t in range(R)]
 
@@ -43,351 +44,276 @@ def rank_program(g, core, T, topo):
     wide = topo.mask(core, nxt)
     lanes = len(topo.engines(core, nxt))
     A, F = AluOpType, ActivationFunctionType
+    V, S = g.vector, g.scalar
 
-    queue = {"v": g.vector, "s": g.scalar, "t": g.tensor, "g": g, "y": g.sync}
-    counter = {"v": "cv", "s": "cs", "t": "ct", "g": "cg"}
+    queue = {"v": V, "s": S, "t": g.tensor, "g": g, "y": g.sync}
     total = {}
     known = {q: {} for q in queue}
     clock = {}
     wrote, read, banks = {}, {}, {}
-
-    def span(r):
-        return range(r[1], r[2], r[3] if len(r) > 3 else 1)
+    steps = {}
 
     def ap(r):
-        if len(r) > 3:
-            return T[r[0]][:, r[1]:r[2]:r[3]]
-        return T[r[0]][:, r[1]:r[2]]
+        if not isinstance(r, tuple):
+            return r
+        return T[r[0]][:, r[1]:r[2]:r[3]] if len(r) > 3 else T[r[0]][:, r[1]:r[2]]
 
-    def wait(q, need):
-        for sem in sorted(need, key=lambda s: -need[s]):
-            val = need[sem]
-            if known[q].get(sem, 0) >= val:
-                continue
-            queue[q].wait_ge(T.sem[sem], val)
-            for s, v in clock[(sem, val)].items():
-                if known[q].get(s, 0) < v:
-                    known[q][s] = v
+    def learn(into, frm):
+        for s, v in frm.items():
+            if into.get(s, 0) < v:
+                into[s] = v
 
-    def issue(q, call, outs, ins, sem=None, step=1):
+    def issue(q, call, outs, ins, sem):
+        held = [r[1] // BANK for r in ins + outs if r[0] == "ps"]
+        outs, ins = [r for r in outs if r[0] != "ps"], [r for r in ins if r[0] != "ps"]
         need = {}
-
-        def after(mark):
-            if mark is not None and need.get(mark[0], 0) < mark[1]:
-                need[mark[0]] = mark[1]
-
-        for r in list(ins) + list(outs):
-            if r[0] == "ps":
-                for oq, mark in banks.get(r[1] // BANK, {}).items():
-                    if oq != q:
-                        after(mark)
-        for r in ins:
-            if r[0] != "ps":
-                w = wrote.get(r[0], {})
-                for c in span(r):
-                    after(w.get(c))
+        for b in held:
+            learn(need, dict(mark for oq, mark in banks.get(b, {}).items() if oq != q))
+        for r in ins + outs:
+            w = wrote.get(r[0], {})
+            for mark in {w[c] for c in range(*r[1:]) if c in w}:
+                learn(need, dict([mark]))
         for r in outs:
-            if r[0] != "ps":
-                w, rd = wrote.get(r[0], {}), read.get(r[0], {})
-                for c in span(r):
-                    after(w.get(c))
-                    for mark in rd.get(c, {}).items():
-                        after(mark)
+            rd = read.get(r[0], {})
+            for c in range(*r[1:]):
+                learn(need, rd.get(c, {}))
         for sa in list(need):
             for sb in list(need):
                 if sa != sb and sa in need and sb in need and clock[(sb, need[sb])].get(sa, 0) >= need[sa]:
                     del need[sa]
-        wait(q, need)
-        sem = sem or counter[q]
+        for s in sorted(need, key=lambda s: -need[s]):
+            if known[q].get(s, 0) < need[s]:
+                queue[q].wait_ge(T.sem[s], need[s])
+                learn(known[q], clock[(s, need[s])])
+        far = sem is not None and sem.startswith("arr")
+        step = 1 if sem is None else 2 * lanes if far else 16
+        sem = sem or "c" + q
         total[sem] = total.get(sem, 0) + step
         mark = (sem, total[sem])
-        ck = dict(clock.get((sem, total[sem] - step), {}))
-        for s, v in known[q].items():
-            if ck.get(s, 0) < v:
-                ck[s] = v
-        ck[sem] = total[sem]
-        clock[mark] = ck
-        call().then_inc(T.sem[sem], step)
-        for r in list(ins) + list(outs):
-            if r[0] == "ps":
-                banks.setdefault(r[1] // BANK, {})[q] = mark
-        for r in ins:
-            if r[0] != "ps":
-                rd = read.setdefault(r[0], {})
-                for c in span(r):
-                    rd.setdefault(c, {})[sem] = total[sem]
+        clock[mark] = dict(clock.get((sem, total[sem] - step), {}))
+        if far:
+            call(q)
+        else:
+            learn(clock[mark], known[q])
+            call(q).then_inc(T.sem[sem], step)
+        clock[mark][sem] = total[sem]
+        for b in held:
+            banks.setdefault(b, {})[q] = mark
+        for r in ([] if far else ins):
+            rd = read.setdefault(r[0], {})
+            for c in range(*r[1:]):
+                rd.setdefault(c, {})[sem] = total[sem]
         for r in outs:
-            if r[0] != "ps":
-                w, rd = wrote.setdefault(r[0], {}), read.setdefault(r[0], {})
-                for c in span(r):
-                    w[c] = mark
-                    rd.pop(c, None)
+            w, rd = wrote.setdefault(r[0], {}), read.setdefault(r[0], {})
+            for c in range(*r[1:]):
+                w[c] = mark
+                rd.pop(c, None)
 
-    def val(x):
-        return ap(x) if isinstance(x, tuple) else x
-
-    def refs(*xs):
-        return [x for x in xs if isinstance(x, tuple)]
+    def step(name, qs, call, outs, ins, sem=None):
+        steps[name] = (qs, call, [r for r in outs if isinstance(r, tuple)], [r for r in ins if isinstance(r, tuple)], sem)
 
     def u8(r):
         return ap(r).bitcast(dt.uint8)
 
-    def memset(out, c):
-        issue("v", lambda: g.vector.memset(ap(out), c), [out], [])
+    def u32(r):
+        return ap(r).bitcast(dt.uint32)
 
-    def ts(out, in0, s1, op0, s2=None, op1=None):
-        if op1 is None:
-            issue("v", lambda: g.vector.tensor_scalar(ap(out), ap(in0), val(s1), None, op0), [out], refs(in0, s1))
-        else:
-            issue("v", lambda: g.vector.tensor_scalar(ap(out), ap(in0), val(s1), val(s2), op0, op1), [out], refs(in0, s1, s2))
+    def ts(name, out, in0, s1, op0, s2=None, op1=None):
+        ops = [op0] if op1 is None else [op0, op1]
+        step(name, "v", lambda q: V.tensor_scalar(ap(out), ap(in0), ap(s1), ap(s2), *ops), [out], [in0, s1, s2])
 
-    def tt(out, in0, in1, op, off=None):
-        if off is None:
-            issue("v", lambda: g.vector.tensor_tensor(ap(out), ap(in0), ap(in1), op), [out], [in0, in1])
-        else:
-            issue("v", lambda: g.vector.tensor_tensor(ap(out), ap(in0).indirect(ap(off)), ap(in1), op), [out], [in0, in1, off])
+    def tt(name, out, in0, in1, op, off=None):
+        step(name, "v", lambda q: V.tensor_tensor(ap(out), ap(in0).indirect(ap(off)) if off else ap(in0), ap(in1), op),
+             [out], [in0, in1, off])
 
-    def copy(out, in_):
-        issue("v", lambda: g.vector.tensor_copy(ap(out), ap(in_)), [out], [in_])
+    def scan(name, out, d0, d1, init, op0, op1):
+        step(name, "v", lambda q: V.tensor_tensor_scan(ap(out), ap(d0), ap(d1), ap(init), op0, op1), [out], [d0, d1, init])
 
-    def scan(out, d0, d1, init, op0, op1):
-        issue("v", lambda: g.vector.tensor_tensor_scan(ap(out), ap(d0), ap(d1), val(init), op0, op1), [out], refs(d0, d1, init))
+    def copy(name, qs, out, in_, off=None):
+        def call(q):
+            src = ap(in_).indirect(ap(off)) if off else ap(in_)
+            if q == "g":
+                return g.affine_select(ap(out), src, [[0, out[2] - out[1]]], A.is_ge, 0.0, 0, 0)
+            return V.tensor_copy(ap(out), src) if q == "v" else S.activation(ap(out), src, F.Copy)
+        step(name, qs, call, [out], [in_, off])
 
-    def pick(q, out, win, off):
-        if q == "v":
-            issue("v", lambda: g.vector.tensor_copy(ap(out), ap(win).indirect(ap(off))), [out], [win, off])
-        else:
-            issue("s", lambda: g.scalar.activation(ap(out), ap(win).indirect(ap(off)), F.Copy), [out], [win, off])
+    def scatter(name, win, off, in_):
+        step(name, "v", lambda q: V.tensor_copy(ap(win).indirect(ap(off)), ap(in_)), [win], [off, in_])
 
-    def scatter(win, off, in_):
-        issue("v", lambda: g.vector.tensor_copy(ap(win).indirect(ap(off)), ap(in_)), [win], [off, in_])
+    def act(name, out, in_, func, **kw):
+        step(name, "s", lambda q: S.activation(ap(out), ap(in_), func, **{k: ap(kw[k]) for k in kw}),
+             [out, kw.get("accum_out")], [in_, kw.get("bias")])
 
-    def act(out, in_, func, bias=None, scale=None, accum=None):
-        kw = {}
-        if scale is not None:
-            kw["scale"] = scale
-        if bias is not None:
-            kw["bias"] = ap(bias)
-        if accum is not None:
-            kw["accum_out"] = ap(accum)
-        issue("s", lambda: g.scalar.activation(ap(out), ap(in_), func, **kw), refs(out, accum), refs(in_, bias))
+    def quant(name, to, in_):
+        step(name, "v", lambda q: V.quantize_mx(ap(to[0]), ap(to[1]), ap(in_)), to, [in_])
 
-    def quant(q, p, in_):
-        issue("v", lambda: g.vector.quantize_mx(ap(q), ap(p), ap(in_)), [q, p], [in_])
+    def bank(b, a=0, e=L):
+        return ("ps", b * BANK + a, b * BANK + e)
 
-    def bank(b):
-        return ("ps", b * BANK, b * BANK + L)
+    def mm(name, b, w, x):
+        out = bank(b, 0, x[0][2] - x[0][1])
+        step(name, "t", lambda q: g.tensor.matmul_mx(ap(out), ap(w[0]), ap(w[1]), ap(x[0]), ap(x[1]), True, True), [out], w + x)
 
-    def mm(b, w, x):
-        issue("t", lambda: g.tensor.matmul_mx(ap(bank(b)), ap(w[0]), ap(w[1]), ap(x[0]), ap(x[1]), True, True), [bank(b)], list(w) + list(x))
+    def iota(name, out, pattern, base, cm=0, **kw):
+        step(name, "g", lambda q: g.iota(ap(out), pattern, base, cm, **kw), [out], [])
 
-    def iota(out, pattern, base, cm, loose=False):
-        if loose:
-            issue("g", lambda: g.iota(ap(out), pattern, base, cm, allow_small_or_imprecise_dtypes=True), [out], [])
-        else:
-            issue("g", lambda: g.iota(ap(out), pattern, base, cm), [out], [])
-
-    def load(q, sem, out, dst, src, behind=()):
-        issue(q, lambda: queue[q].dma_start(dst, src), [out], list(behind), sem, 16)
-
-    def store(q, dst, src, in_):
-        issue(q, lambda: queue[q].dma_start(dst, src), [], [in_], "dout", 16)
-
-    def whole(name):
-        return (name, 0, SCRATCH[name][1][1])
+    def dma(name, qs, sem, dst, src, outs, ins):
+        step(name, qs, lambda q: queue[q].dma_start(dst, src), outs, ins, sem)
 
     def plane(name, t, a, b):
         w = SCRATCH[name][1][1] // 4
         return (name, t * w + a, t * w + b)
 
-    def side(q, p, b):
-        return (q, 128 * b, 128 * b + 128), (p, 128 * b, 128 * b + 128)
+    def side(name, b=0, n=128):
+        return (name + "q", n * b, n * b + n), (name + "p", n * b, n * b + n)
 
     PC = C // 16
-    col_c, col_a = ("cols", 0, 1), ("cols", 1, 2)
-    qz, qu, qur = (whole("zq"), whole("zp")), (whole("uq"), whole("up")), (whole("urq"), whole("urp"))
-    SV, SS, LAY, DEC = 0, 1, (2, 3), (4, 5, 6, 7)
+    W = {n: (n, 0, SCRATCH[n][1][1]) for n in SCRATCH}
+    loose = {"allow_small_or_imprecise_dtypes": True}
+    col_c, col_a, col_e, col_m = (("cols", i, i + 1) for i in range(4))
+    pm, pi = ("pm", 0, 1), ("pi", 0, 1)
+    qz, qu, qur = side("z", 0, L), side("u"), side("ur")
+    SV, SS, LAY, DEC = 0, 1, (2, 3, 4, 5), (6, 7, 2, 3)
 
-    load("y", "dx", whole("xs"), T.xs[:], T.x[:])
-    load("s", "dpar", whole("pari"), T.pari[:], T.par[:])
-    load("s", "dtop", whole("topi"), T.topi[:], T.top[:])
-    load("y", "du", whole("us"), T.us[:], T.u[:])
-    load("y", "dwc", whole("wq"), u8(whole("wq")), T.wc[:], [("xs", 0, 1)])
-    load("y", "dws", whole("wp"), T.wp[:], T.ws[:])
+    dma("lx", "y", "dx", T.xs[:], T.x[:], [W["xs"]], [])
+    dma("lp", "s", "dpar", T.pari[:], T.par[:], [W["pari"]], [])
+    dma("lt", "s", "dtop", T.topi[:], T.top[:], [W["topi"]], [])
+    dma("lu", "y", "du", T.us[:], T.u[:], [W["us"]], [])
+    dma("lw", "y", "dwc", u8(W["wq"]), T.wc[:], [W["wq"]], [("xs", 0, 1)])
+    dma("ls", "y", "dws", T.wp[:], T.ws[:], [W["wp"]], [("xs", 0, 1)])
 
-    iota(whole("di"), [[0, K], [-1, 16]], 16, 1)
-    iota(("pt", 0, C), [[1, C]], 0, 0, True)
-    iota(whole("ui"), [[16, 8]], 0, 0)
-    iota(whole("ni"), [[-L, R], [16, K]], -L, 0)
-    memset(whole("ones"), 1.0)
-    memset(whole("ar"), 9.0e29)
-    memset(whole("rz"), 1.0)
-    for k in range(DS):
-        memset(("sg", k * SEG + L, k * SEG + L + 1), -16.0 * k)
-    memset(("ar", 0, L, 16), -9.0e29)
-    memset(("rz", 0, L, 16), 0.0)
-    issue("g", lambda: g.affine_select(T.eb[:], T.ones[:], [[-1, 520]], A.is_equal, 0.0, 3, 4), [whole("eb")], [whole("ones")])
-    ts(whole("dm"), whole("di"), 15, A.bitwise_and)
-    ts(whole("mk"), whole("dm"), 0.5, A.subtract, -BIG, A.mult)
-    for t in range(4):
-        ts(("par4", t * PC, (t + 1) * PC), whole("pari"), 4.0, A.mult, float(t), A.add)
-    copy(whole("paru"), whole("pari"))
-    copy(("topu", 0, K), whole("topi"))
-    pick("s", ("pt", NODES, NODES + C), ("pt", 0, C), whole("paru"))
-    pick("s", ("pt", NODES + C, NODES + C + L), ("pt", 0, C), ("topu", 0, K))
-    ts(col_c, ("dm", 0, 1), 15.0, A.subtract, -HOLD, A.mult)
-    ts(col_a, ("dm", 0, 1), 1.0 - HOLD, A.mult, 15.0 * HOLD, A.add)
-    copy(whole("uo"), whole("ui"))
-    ts(whole("ax"), whole("mk"), -1.0, A.mult, HOLD, A.min)
-    ts(whole("newc"), whole("ni"), col_a, A.add)
-    ts(whole("x15"), whole("topi"), col_c, A.add)
+    iota("ip", pi, [[0, 1]], 0, 1)
+    iota("ii", W["ir"], [[0, K], [1, 16]], 0, **loose)
+    iota("iu", W["ui"], [[16, 12]], 0)
+    iota("in", W["ni"], [[-L, R], [16, K]], -L)
+    step("one", "v", lambda q: V.memset(T.ones[:], 1.0), [W["ones"]], [])
+    ts("pm", pm, pi, 15, A.bitwise_and)
+    scan("cum", ("pt", 0, 520), W["ones"], W["ones"], -1.0, A.add, A.mult)
+    ts("ce", col_e, pi, 4.0, A.mult, 3.0, A.add)
+    ts("cm", col_m, pm, -BIG, A.mult)
+    ts("eb", W["eb"], ("pt", 0, 520), col_e, A.is_equal)
+    act("mk", W["mk"], W["ir"], F.Abs, bias=col_m, scale=BIG)
+    act("ar", W["ar"], W["ir"], F.Identity, bias=-3.0e28, scale=6.0e28)
+    act("rz", W["rz"], W["ir"], F.Sign)
     for b in range(4):
-        quant(side("eq", "ep", b)[0], side("eq", "ep", b)[1], ("eb", 3 - b, 515 - b))
-
-    def first_top(t):
-        pick("s", plane("at", t, 0, L), plane("pool", t, 0, C), ("topu", 0, K))
-
-    copy(plane("pool", 0, 0, C), ("xs", 0, 4 * C, 4))
-    act(plane("pool", 1, 0, C), ("xs", 1, 4 * C, 4), F.Copy)
-    for t in (2, 3):
-        issue("g", lambda: g.affine_select(ap(plane("pool", t, 0, C)), ap(("xs", t, 4 * C, 4)), [[0, C]], A.is_ge, 0.0, 0, 0),
-              [plane("pool", t, 0, C)], [("xs", t, 4 * C, 4)])
-    iota(("pt", NODES - L, NODES), [[1, L]], C, 0, True)
-    first_top(0)
+        quant("qe%d" % b, side("e", b), ("eb", 3 - b, 515 - b))
+    ts("cc", col_c, pm, 15.0, A.subtract, -HOLD, A.mult)
+    ts("ca", col_a, pm, 1.0 - HOLD, A.mult, 15.0 * HOLD, A.add)
+    copy("uo", "v", W["uo"], ("ui", 0, 8))
+    ts("sk", ("sg", L, DS * SEG, SEG), ("ui", 0, DS), -1.0, A.mult)
+    ts("nw", W["newc"], W["ni"], col_a, A.add)
+    copy("pu", "v", W["paru"], W["pari"])
     for t in range(4):
-        tt(plane("vt", t, 0, C), whole("xs"), plane("pool", t, 0, C), A.add, ("par4", t * PC, (t + 1) * PC))
-        if t == 1:
-            quant(qu[0], qu[1], whole("us"))
-    for t in range(3):
-        pick("s", ("z", t, 4 * L, 4), plane("vt", t, 0, C), ("topu", 0, K))
-        if t == 1:
-            pick("s", qur[1], qu[1], whole("uo"))
-    pick("v", ("z", 3, 4 * L, 4), plane("vt", 3, 0, C), ("topu", 0, K))
+        ts("p4%d" % t, ("par4", t * PC, (t + 1) * PC), W["pari"], 4.0, A.mult, float(t), A.add)
+    copy("tu", "v", ("topu", 0, K), W["topi"])
+    ts("x15", W["x15"], W["topi"], col_c, A.add)
+    copy("pp", "sv", ("pt", NODES, NODES + C), ("pt", 0, C), W["paru"])
+    copy("pt", "sv", ("pt", NODES + C, NODES + C + L), ("pt", 0, C), ("topu", 0, K))
+    iota("n0", ("pt", NODES - L, NODES), [[1, L]], C, **loose)
+    ts("ax", W["ax"], W["mk"], DROP + HOLD, A.min, DROP, A.subtract)
+
+    for t in range(4):
+        copy("pl%d" % t, ("vsg", "svg", "gsv", "gsv")[t], plane("pool", t, 0, C), ("xs", t, 4 * C, 4))
+    for t in range(4):
+        tt("vt%d" % t, plane("vt", t, 0, C), W["xs"], plane("pool", t, 0, C), A.add, ("par4", t * PC, (t + 1) * PC))
+    quant("qu", qu, W["us"])
+    step("uq", "v", lambda q: V.tensor_copy(u32(qur[0]), u32(qu[0]).indirect(T.uo[:])), [qur[0]], [qu[0], W["uo"]])
+    copy("up", "sv", qur[1], qu[1], W["uo"])
+    iota("n1", ("pt", C, NODES - L), [[-L, R - 1], [1, L]], NODES - L, **loose)
+
+    def reading(r):
+        n = L // ZH[r]
+        for i in range(ZH[r]):
+            for t in range(4):
+                copy("z%d%d%d" % (r, i, t), "vs" if t > 1 else "sv", ("z", 4 * n * i + t, 4 * n * (i + 1), 4),
+                     plane("vt", t, 0, C + L * r), ("topu", r * K + i * n // 16, r * K + (i + 1) * n // 16))
+            quant("qz%d%d" % (r, i), side("z", i, n), ("z", 4 * n * i, 4 * n * (i + 1)))
+
+    def one_round(r):
+        have, ds, n = C + L * r, DSS[r], str(r)
+        held = W["x15"] if r == 0 else ("xx", 15, L, 16)
+        hq, hp, lq, lp = (W[b + n] for b in ("hq", "hp", "lq", "lp"))
+        reading(r)
+        for t in range(4):
+            copy("a%d%d" % (r, t), "sv", plane("at", t, 0, L), plane("pool", t, 0, have), ("topu", r * K, (r + 1) * K))
+        mm("mv" + n, SV, qur, qz)
+        mm("ms" + n, SS, qur, qz)
+        for b in range(4):
+            mm("ml%d%d" % (r, b), LAY[b], side("w", b), qz)
+            act("h%d%d" % (r, b), ("h", b, 4 * L, 4), bank(LAY[b]), F.Relu, scale=0.015625)
+
+        for i in range(2):
+            a, e = i * M, (i + 1) * M
+            tt("bm%d%d" % (r, i), ("bm", a, e), bank(SV, a, e), ("mk", a, e), A.subtract)
+            scan("ff%d%d" % (r, i), ("ff", a, e), ("ar", a, e), ("bm", a, e), 0.0, A.min, A.max)
+
+        ts("t1" + n, W["t1"], ("ff", 15, L, 16), 0.0, A.is_ge, -BIG, A.mult)
+        tt("ne" + n, W["ne"], bank(SV), W["ff"], A.not_equal)
+        tt("t2" + n, W["t2"], W["t1"], held, A.add)
+        scan("nc" + n, W["nc"], W["rz"], W["ne"], 0.0, A.mult, A.add)
+        tt("t3" + n, W["t3"], W["t2"], ("newc", r * K, (r + 1) * K), A.max)
+        ts("ix" + n, W["idx"], W["t3"], col_c, A.subtract, float(L * (r + 1)), A.add)
+        ts("sn" + n, ("sg", L + 1, ds * SEG, SEG), ("nc", 15, 16 * ds, 16), -1.0, A.mult)
+        quant("qh" + n, (hq, hp), W["h"])
+
+        def hand_on(q):
+            g.remote_dma(u8(lq), u8(hq), T.sem["arr" + n], T.sem.sent, pid, rid, wide)
+            g.remote_dma(ap(lp), ap(hp), T.sem["arr" + n], T.sem.sent, pid, rid, wide)
+        step("go" + n, "g", hand_on, [lq, lp], [hq, hp], "arr" + n)
+        copy("nr" + n, "sv", W["nrow"], ("pt", NODES - L * (r + 1), NODES + have), W["idx"])
+
+        for k in range(K):
+            own, cut, c = ("ff", 16 * k + 15, 16 * k + 16), 16 * k + 16, n + chr(97 + k)
+            if k < ds:
+                j = k * SEG
+                act("S" + c, ("sg", j, j + L), bank(SS), F.Sign, bias=own, scale=-1.0)
+                act("B" + c, ("sj", j, j + cut), ("sg", j, j + cut), F.Relu, accum_out=("acc", k, k + 1))
+                act("A" + c, ("sj", j + cut, j + L + 2), ("sg", j + cut, j + L + 2), F.Relu, scale=-1.0,
+                    accum_out=("acc", K + k, K + k + 1))
+            else:
+                j, o = (k - ds) * L, (k - ds) * M
+                ts("E" + c, ("fl", j, j + cut), bank(SV, 0, cut), own, A.is_ge, 0.5, A.subtract)
+                if cut < L:
+                    ts("G" + c, ("fl", j + cut, j + L), bank(SV, cut, L), own, A.is_gt, 0.5, A.subtract)
+                scan("C" + c, ("fs", o, o + M), ("fl", j, j + M), ("fl", j + M, j + L), ("nc", cut - 1, cut), A.add, A.add)
+
+        order = ("pt", NODES + have + L, NODES + have + 2 * L)
+        ts("rv" + n, ("rv", 0, K - ds), ("fs", M - 1, (K - ds) * M, M), M - 16.0, A.add)
+        scatter("sv" + n, order, ("rv", 0, K - ds), ("nrow", 16 * ds, L))
+        tt("c1" + n, ("c1", 0, ds), ("acc", K, K + ds), ("acc", 0, ds), A.subtract)
+        copy("rs" + n, "v", ("rs", 0, ds), ("c1", 0, ds))
+        scatter("ss" + n, order, ("rs", 0, ds), ("nrow", 0, 16 * ds))
+        for b in range(4):
+            mm("md%d%d" % (r, b), DEC[b], side("e", b), (lq, lp))
+        for b in range(4):
+            if r + 1 < R:
+                copy("d%d%d" % (r, b), "s", plane("pool", b, have, have + L), bank(DEC[b]))
+            tt("w%d%d" % (r, b), plane("vt", b, have, have + L), bank(DEC[b]), plane("at", b, 0, L), A.add)
+        for i in range(2):
+            a, e = i * M, (i + 1) * M
+            scan("xx%d%d" % (r, i), ("xx", a, e), ("ax", a, e), ("pt", order[1] + a, order[1] + e), 0.0, A.add, A.max)
+            ts("to%d%d" % (r, i), ("topu", (r + 1) * K + a // 16, (r + 1) * K + e // 16), ("xx", a + 15, e, 16), col_c, A.subtract)
+        if r + 1 == R:
+            dma("ol", "y", "dout", T.ol[:], T.pt[0:128:16, order[1]:order[2]], [], [order])
 
     for r in range(R):
-        have = C + L * r
-        ds = DSS[r]
-        tops = ("topu", r * K, (r + 1) * K)
-        held = whole("x15") if r == 0 else ("xx", 15, L, 16)
-        hq, hp, lq, lp = (whole(n % r) for n in ("hq%d", "hp%d", "lq%d", "lp%d"))
-        later = list(range(4)) if r > 0 else []
+        one_round(r)
 
-        def old_top(q):
-            if later:
-                t = later.pop(0)
-                pick(q, plane("at", t, 0, L), plane("pool", t, 0, have), tops)
-
-        quant(qz[0], qz[1], whole("z"))
-        old_top("s")
-        old_top("v")
-        if r == 0:
-            first_top(1)
-            issue("v", lambda: g.vector.tensor_copy(T.urq[:].bitcast(dt.uint32), T.uq[:].bitcast(dt.uint32).indirect(T.uo[:])),
-                  [qur[0]], [qu[0], whole("uo")])
-        else:
-            mm(SV, qur, qz)
-        for b in range(4):
-            mm(LAY[b % 2], side("wq", "wp", b), qz)
-            if b == 0 and r == 0:
-                mm(SV, qur, qz)
-            if b == 1:
-                mm(SS, qur, qz)
-            act(("h", b, 4 * L, 4), bank(LAY[b % 2]), F.Relu, scale=0.015625)
-
-        tt(whole("bm"), bank(SV), whole("mk"), A.min)
-        scan(whole("ff"), whole("ar"), whole("bm"), 0.0, A.min, A.max)
-
-        def own(k):
-            return ("ff", 16 * k + 15, 16 * k + 16)
-
-        def compare(k):
-            j, cut = (k - ds) * L, 16 * k + 16
-            ts(("fl", j, j + cut), ("ps", SV * BANK, SV * BANK + cut), own(k), A.is_ge, 0.5, A.subtract)
-            if cut < L:
-                ts(("fl", j + cut, j + L), ("ps", SV * BANK + cut, SV * BANK + L), own(k), A.is_gt, 0.5, A.subtract)
-
-        def count(k):
-            j, o, m = (k - ds) * L, (k - ds) * (L // 2), L // 2
-            scan(("fs", o, o + m), ("fl", j, j + m), ("fl", j + m, j + L), ("nc", 16 * k + 15, 16 * k + 16), A.add, A.add)
-
-        def signs(k):
-            act(("sg", k * SEG, k * SEG + L), bank(SS), F.Sign, bias=own(k), scale=-1.0)
-
-        def sums(k):
-            j, cut = k * SEG, 16 * k + 16
-            act(("sj", j, j + cut), ("sg", j, j + cut), F.Relu, accum=("acc", k, k + 1))
-            act(("sj", j + cut, j + L + 2), ("sg", j + cut, j + L + 2), F.Relu, scale=-1.0, accum=("acc", K + k, K + k + 1))
-
-        ts(whole("t1"), ("ff", 15, L, 16), 0.0, A.is_ge, -BIG, A.mult)
-        tt(whole("ne"), bank(SV), whole("ff"), A.not_equal)
-        tt(whole("t2"), whole("t1"), held, A.add)
-        compare(ds)
-        quant(hq, hp, whole("h"))
-        wait("g", {"cv": total["cv"]})
-        g.remote_dma(u8(lq), u8(hq), T.sem["arr%d" % r], T.sem.sent, pid, rid, wide)
-        g.remote_dma(ap(lp), ap(hp), T.sem["arr%d" % r], T.sem.sent, pid, rid, wide)
-        mark = ("arr%d" % r, 2 * lanes)
-        clock[mark] = {mark[0]: mark[1]}
-        wrote[lq[0]] = {c: mark for c in span(lq)}
-        wrote[lp[0]] = {c: mark for c in span(lp)}
-        tt(whole("t3"), whole("t2"), ("newc", r * K, (r + 1) * K), A.max)
-        scan(whole("nc"), whole("rz"), whole("ne"), 0.0, A.mult, A.add)
-        ts(whole("idx"), whole("t3"), col_c, A.subtract, float(L * (r + 1)), A.add)
-        ts(("sg", L + 1, ds * SEG, SEG), ("nc", 15, 16 * ds, 16), -1.0, A.mult)
-        if r == 0:
-            iota(("pt", C, NODES - L), [[-L, R - 1], [1, L]], NODES - L, 0, True)
-
-        signs(0)
-        signs(1)
-        pick("s", whole("nrow"), ("pt", NODES - L * (r + 1), NODES + have), whole("idx"))
-        for k in range(ds):
-            if 1 < k + 1 < ds:
-                signs(k + 1)
-            sums(k)
-            old_top("s")
-            if r == 0 and k < 2:
-                first_top(2 + k)
-        for k in range(ds, K):
-            if k + 1 < K:
-                compare(k + 1)
-            count(k)
-
-        for b in range(4):
-            mm(DEC[b], side("eq", "ep", b), (lq, lp))
-        order = ("pt", NODES + have + L, NODES + have + 2 * L)
-        fresh = [0, 1, 2, 3]
-
-        def new_sum():
-            b = fresh.pop(0)
-            tt(plane("vt", b, have, have + L), bank(DEC[b]), plane("at", b, 0, L), A.add)
-
-        ts(("rv", 0, K - ds), ("fs", L // 2 - 1, (K - ds) * (L // 2), L // 2), L // 2 - 16.0, A.add)
-        scatter(order, ("rv", 0, K - ds), ("nrow", 16 * ds, L))
-        while len(fresh) > LATE[r]:
-            new_sum()
-        tt(("c1", 0, ds), ("acc", K, K + ds), ("acc", 0, ds), A.subtract)
-        copy(("rs", 0, ds), ("c1", 0, ds))
-        scatter(order, ("rs", 0, ds), ("nrow", 0, 16 * ds))
-        if r + 1 < R:
-            for b in range(4):
-                act(plane("pool", b, have, have + L), bank(DEC[b]), F.Copy)
-        scan(whole("xx"), whole("ax"), order, 0.0, A.add, A.max)
-        moved = ("topu", (r + 1) * K, (r + 2) * K)
-        ts(moved, ("xx", 15, L, 16), col_c, A.subtract)
-        while fresh:
-            new_sum()
-        if r + 1 == R:
-            store("y", T.ol[:], T.pt[0:128:16, order[1]:order[2]], order)
-        for t in range(4):
-            pick("s" if t < (3 if LATE[r] > 1 else 2) else "v", ("z", t, 4 * L, 4), plane("vt", t, 0, have + L), moved)
-
-    quant(qz[0], qz[1], whole("z"))
-    mm(SS, qu, qz)
-    store("y", T.oc[:], u8(qz[0]), qz[0])
-    copy(whole("ys"), bank(SS))
+    reading(R)
+    dma("oc", "y", "dout", T.oc[:], u8(qz[0]), [], [qz[0]])
     for k in range(4):
-        store("s", T.osc[4 * k:4 * k + 4, :], T.zp[32 * k:32 * k + 4, :], qz[1])
-    store("y", T.y[:], T.ys[:], whole("ys"))
+        dma("os%d" % k, "ys", "dout", T.osc[4 * k:4 * k + 4, :], T.zp[32 * k:32 * k + 4, :], [], [qz[1]])
+    for i in range(2):
+        half = ("ys", i * M, (i + 1) * M)
+        mm("my%d" % i, i, qu, side("z", i, M))
+        copy("y%d" % i, ("vs", "sv")[i], half, bank(i, 0, M))
+        dma("oy%d" % i, ("ys", "sy")[i], "dout", T.y[:, i * M:(i + 1) * M], ap(half), [], [half])
+
+    for name in ORDER.split() or list(steps):
+        name, _, q = name.partition(".")
+        qs, call, outs, ins, sem = steps.pop(name)
+        issue(q or qs[0], call, outs, ins, sem)
+    assert not steps
 
     g.wait_ge(T.sem.sent, 2 * lanes * R)
     for sem in sorted(total):

@@ -7,7 +7,7 @@ K = L // 16
 M = L // 2
 DSS = (7, 7, 7)
 ZH = (1, 2, 2, 2)
-ORDER = "lx ip one lt lp lu ii ce pm cum n0 cm eb mk ar ca iu qe2 rz in qe1 qe0 n1 pu cc qe3 pp tu p40 sk p42 uo ax nw x15 pl0 pl1 pl2 ls lw p41 p43 vt0 pt pl3 a01 vt1 z000 qu a02 vt2 vt3 z002.s z001 up.v z003 a00 uq qz00 a03 mv0 ml00 ml01 bm00 ml02 h00 bm01 ml03 ff00 ms0 h01 ff01 G0i h02 E0j ne0 h03 G0h S0g nc0 t10 E0h S0e qh0 S0d G0j C0h go0 S0f E0n t20 G0s S0b E0o t30 B0f E0q B0d S0c sn0 E0k ix0 B0b E0s A0g B0g E0l S0a G0r C0j G0n A0e G0k G0m A0d G0l G0o E0i A0b C0s E0p B0c A0c G0q C0l E0m A0f C0n E0r B0e B0a A0a E0t C0m nr0 G0p C0i C0k C0p C0t C0q C0o C0r c10 md00 rv0 rs0 md02 sv0 md01 md03 d02 d03 w00 d01 ss0 d00 w02 xx01 xx00 to01 to00 w03 z110 z100 w01 z112.s z102 z113 z111 z103 z101 qz11 a13 qz10 a10.v mv1 a11 ml11 ml10 bm11 ml12 bm10 a12 ml13 ff11 ms1 ff10 E1l h10 ne1 h12 t11 G1h E1h h13 G1q E1k h11 t21 G1i G1j S1c qh1 S1f G1k nc1 go1 S1g E1i G1s E1q S1b t31 S1d G1l C1i sn1 E1t S1a E1o A1f E1r S1e E1j B1b ix1 B1g G1n B1e G1o C1j A1g G1r G1p E1p nr1 G1m E1n A1e C1q C1l C1k B1c E1m B1a A1b C1p E1s B1d md11 A1d C1m C1o md13 C1s C1t A1c md12 C1h C1n md10 C1r B1f w13 A1a rv1 d12 c11 sv1 d10 d13 rs1 w11 ss1 d11 xx10 xx11 to10 w10 z201 to11 w12 z213.s z203 z210 z212 z211 z202 z200 qz21 a23 qz20 a20.v mv2 a21 ml22 ml21 bm21 ml23 bm20 a22 ml20 ff21 ms2 ff20 G2o ne2 h21 G2i h20 nc2 E2p h23 E2h h22 E2j G2h S2c t12 G2m qh2 S2e G2r S2d E2m go2 E2l S2a G2q E2s B2c S2b G2l G2n C2h S2g E2n G2p B2b E2k B2g G2j B2e t22 E2i S2f sn2 E2o A2d G2s C2j t32 A2a G2k E2q B2d B2a C2o A2g C2n C2i E2r A2b ix2 A2f E2t A2c C2q C2t md23 C2k A2e C2l md21 C2p C2s md20 B2f C2r C2m nr2 md22 w23 rv2 c12 w20 sv2 rs2 ss2 w22 xx21 xx20 to21 w21 z310 z313 z311 to20 z312 z301 z302 z300 z303 qz31 qz30 my1 my0 oc y1 os3 os2 y0.s ol os1.s oy1.y oy0.s os0"
+ORDER = "lx ip lt one ii lp pb ce pm cum iu cm cc sm in eb ar mk sk uo qe1 tu ay x15 cr qe0 qe2 pt qe3 p40 p41 ca pl1 pl0 pl2 lu pu lw p42 p43 vt0 t20 ls ax a01 vt1 pl3 pp vt2 z000 n0 vt3 z002.s qu z003 z001 uq up qz00 a03 nw a00.v mv0 a02 ml00 bm00 ml01 bm01 h00 ml02 ff00 ml03 h01 ff01 ms0 G0i h02 ne0 h03 E0h G0r nc0 t00 S0d G0l G0q qh0 S0b G0j S0c G0h go0 sn0 E0s S0e G0s S0g C0h E0j E0o B0c S0a G0k E0k t10 A0b E0i E0m A0g E0n A0e G0o G0n S0f G0p E0r A0d C0n G0m A0f C0k C0i B0b E0p B0e B0d E0q A0a C0s B0a E0l A0c C0q t30 B0f E0t B0g n1 C0p ix0 C0r C0o C0t nr0 C0l C0m C0j c10 rs0 ss0 md03 md00 md02 d03 md01 w00 d02 xx01 d01 xx00 to01 w02 d00 to00 z110 w03 z100 w01 z112.s z113 z111 z101.v z102.s z103 a13 qz11 qz10 a10.v t21 a11 mv1 ml10 ml12 bm11 bm10 ml11 h10 ff11 ml13 ff10 h12 ms1 E1k h11 G1i G1s G1k t01 h13 ne1 S1e E1h G1j S1d nc1 qh1 S1a E1t sn1 S1b go1 E1i B1a E1q A1d E1j t11 B1b S1g E1l G1h S1f E1m A1a G1r E1o G1p S1c E1p A1e G1l E1n A1c t31 C1i G1m A1f G1q C1p E1s A1g B1f G1o B1c C1j B1g C1s C1k B1e C1h md11 B1d ix1 C1m A1b md13 C1l E1r md12 nr1 md10 G1n C1q C1r d12 C1o C1t C1n c11 d10 w13 a12 rs1 w11 ss1 d13 d11 w10 xx10 xx11 to10 w12 t22 z200 to11 z203 z210 z211.v z213.s z212 z201 z202 a21 qz21 qz20 a20.v a22 mv2 ml21 ml20 bm21 bm20 ml22 h21 ff21 ms2 ff20 h20 ml23 E2p h22 ne2 S2g E2h E2q S2c E2l h23 E2t S2a G2p G2j S2e G2o nc2 qh2 S2b E2j sn2 S2f G2h go2 B2a E2i A2a G2l C2p B2c G2r E2r t02 B2g B2b G2q t12 A2g E2m C2l S2d E2n B2f G2i A2f G2m t32 G2n B2e G2s B2d E2s A2e E2o A2d G2k A2c C2n C2h C2o A2b C2i E2k C2t C2s md20 ix2 C2r C2q md22 C2k nr2 C2m md21 C2j c12 md23 w20 a23 rs2 w22 ss2 w21 ol xx21 xx20 to21 w23 z310 z312 z311 to20 z313 z303.s z302 z301 qz31 z300.v oc1.s my1 qz30 y1 my0 oc0 os2.s os0 oy1 y0 os3 oy0 os1"
 DS, DV = max(DSS), K - min(DSS)
 SEG = L + 8
 BIG = 2.0 ** 93
@@ -17,12 +17,12 @@ BANK = 512
 CODES = "float8_e4m3fn_x4"
 
 WIDTHS = {
-    "bfloat16": {"xs": 4 * C, "us": 512, "ones": 520, "eb": 520, "rz": L, "pool": 4 * HELD, "vt": 4 * NODES, "at": 4 * L,
-                 "z": 4 * L, "h": 4 * L, "ne": L, "nc": L, "fl": DV * L, "fs": DV * M, "sg": DS * SEG, "sj": DS * SEG},
-    "float32": {"ir": L, "mk": L, "ar": L, "ax": L, "cols": 8, "newc": R * K, "x15": K, "pt": 2 * NODES + L, "bm": L, "ff": L,
-                "t1": K, "t2": K, "t3": K, "nrow": L, "acc": 2 * K, "c1": K, "xx": L, "ys": L},
+    "bfloat16": {"xs": 4 * C, "us": 512, "ones": 520, "eb": 520, "ir": L, "pool": 4 * HELD, "vt": 4 * NODES, "at": 4 * L,
+                 "z": 4 * L, "h": 4 * L, "ne": L, "nc": L, "fl": DV * L, "fs": K * M, "sg": (DS + 1) * SEG, "sj": (DS + 1) * SEG},
+    "float32": {"mk": L, "ar": L, "ax": L, "cols": 8, "newc": 2 * R * K, "pp": 2 * K, "x15": K, "pt": 2 * NODES + L,
+                "bm": L, "ff": L, "t0": K, "t3": 2 * K, "nrow": L, "acc": 2 * K, "xx": L, "ys": L},
     "int32": {"pari": C // 16, "topi": K, "ui": 12, "pi": 2, "pm": 2, "ni": R * K},
-    "uint16": {"uo": 8, "paru": C // 16, "par4": 4 * (C // 16), "topu": (R + 1) * K, "idx": K, "rv": K, "rs": K},
+    "uint16": {"uo": 8, "paru": C // 16, "par4": 4 * (C // 16), "topu": (R + 1) * K, "idx": K, "rv": K},
     CODES: {"wq": 512, "uq": 128, "urq": 128, "eq": 512, "zq": L},
     "uint8": {"wp": 512, "up": 128, "urp": 128, "ep": 512, "zp": L},
 }
@@ -118,6 +118,9 @@ def rank_program(g, core, T, topo):
     def u32(r):
         return ap(r).bitcast(dt.uint32)
 
+    def memset(name, out, c):
+        step(name, "v", lambda q: V.memset(ap(out), c), [out], [])
+
     def ts(name, out, in0, s1, op0, s2=None, op1=None):
         ops = [op0] if op1 is None else [op0, op1]
         step(name, "v", lambda q: V.tensor_scalar(ap(out), ap(in0), ap(s1), ap(s2), *ops), [out], [in0, s1, s2])
@@ -178,7 +181,7 @@ def rank_program(g, core, T, topo):
     dma("lx", "y", "dx", T.xs[:], T.x[:], [W["xs"]], [])
     dma("lp", "s", "dpar", T.pari[:], T.par[:], [W["pari"]], [])
     dma("lt", "s", "dtop", T.topi[:], T.top[:], [W["topi"]], [])
-    dma("lu", "y", "du", T.us[:], T.u[:], [W["us"]], [])
+    dma("lu", "y", "du", T.us[:], T.u[:], [W["us"]], [("xs", 0, 1)])
     dma("lw", "y", "dwc", u8(W["wq"]), T.wc[:], [W["wq"]], [("xs", 0, 1)])
     dma("ls", "y", "dws", T.wp[:], T.ws[:], [W["wp"]], [("xs", 0, 1)])
 
@@ -186,7 +189,7 @@ def rank_program(g, core, T, topo):
     iota("ii", W["ir"], [[0, K], [1, 16]], 0, **loose)
     iota("iu", W["ui"], [[16, 12]], 0)
     iota("in", W["ni"], [[-L, R], [16, K]], -L)
-    step("one", "v", lambda q: V.memset(T.ones[:], 1.0), [W["ones"]], [])
+    memset("one", W["ones"], 1.0)
     ts("pm", pm, pi, 15, A.bitwise_and)
     scan("cum", ("pt", 0, 520), W["ones"], W["ones"], -1.0, A.add, A.mult)
     ts("ce", col_e, pi, 4.0, A.mult, 3.0, A.add)
@@ -194,14 +197,16 @@ def rank_program(g, core, T, topo):
     ts("eb", W["eb"], ("pt", 0, 520), col_e, A.is_equal)
     act("mk", W["mk"], W["ir"], F.Abs, bias=col_m, scale=BIG)
     act("ar", W["ar"], W["ir"], F.Identity, bias=-3.0e28, scale=6.0e28)
-    act("rz", W["rz"], W["ir"], F.Sign)
     for b in range(4):
         quant("qe%d" % b, side("e", b), ("eb", 3 - b, 515 - b))
     ts("cc", col_c, pm, 15.0, A.subtract, -HOLD, A.mult)
     ts("ca", col_a, pm, 1.0 - HOLD, A.mult, 15.0 * HOLD, A.add)
     copy("uo", "v", W["uo"], ("ui", 0, 8))
-    ts("sk", ("sg", L, DS * SEG, SEG), ("ui", 0, DS), -1.0, A.mult)
-    ts("nw", W["newc"], W["ni"], col_a, A.add)
+    ts("sk", ("sg", L + SEG, (DS + 1) * SEG, SEG), ("ui", 0, DS), -1.0, A.mult)
+    memset("sm", ("sg", SEG - 1, (DS + 1) * SEG, SEG), M - 16.0)
+    ts("nw", ("newc", 1, 2 * R * K, 2), W["ni"], col_a, A.add, -1.0, A.mult)
+    memset("pb", ("pp", 0, 2 * K, 2), BIG)
+    ts("cr", ("cols", 4, 4 + R), ("ni", 0, R * K, K), col_c, A.add)
     copy("pu", "v", W["paru"], W["pari"])
     for t in range(4):
         ts("p4%d" % t, ("par4", t * PC, (t + 1) * PC), W["pari"], 4.0, A.mult, float(t), A.add)
@@ -210,7 +215,8 @@ def rank_program(g, core, T, topo):
     copy("pp", "sv", ("pt", NODES, NODES + C), ("pt", 0, C), W["paru"])
     copy("pt", "sv", ("pt", NODES + C, NODES + C + L), ("pt", 0, C), ("topu", 0, K))
     iota("n0", ("pt", NODES - L, NODES), [[1, L]], C, **loose)
-    ts("ax", W["ax"], W["mk"], DROP + HOLD, A.min, DROP, A.subtract)
+    act("ay", W["bm"], W["mk"], F.Sign)
+    act("ax", W["ax"], W["bm"], F.Identity, bias=-DROP, scale=DROP + HOLD)
 
     for t in range(4):
         copy("pl%d" % t, ("vsg", "svg", "gsv", "gsv")[t], plane("pool", t, 0, C), ("xs", t, 4 * C, 4))
@@ -247,13 +253,14 @@ def rank_program(g, core, T, topo):
             tt("bm%d%d" % (r, i), ("bm", a, e), bank(SV, a, e), ("mk", a, e), A.subtract)
             scan("ff%d%d" % (r, i), ("ff", a, e), ("ar", a, e), ("bm", a, e), 0.0, A.min, A.max)
 
-        ts("t1" + n, W["t1"], ("ff", 15, L, 16), 0.0, A.is_ge, -BIG, A.mult)
+        act("t0" + n, W["t0"], ("ff", 15, L, 16), F.Sign, bias=2.0 ** -124)
+        act("t1" + n, ("pp", 1, 2 * K, 2), W["t0"], F.Relu, scale=BIG)
+        act("t2" + n, ("newc", 2 * r * K, 2 * (r + 1) * K, 2), held, F.Copy, scale=-1.0)
         tt("ne" + n, W["ne"], bank(SV), W["ff"], A.not_equal)
-        tt("t2" + n, W["t2"], W["t1"], held, A.add)
-        scan("nc" + n, W["nc"], W["rz"], W["ne"], 0.0, A.mult, A.add)
-        tt("t3" + n, W["t3"], W["t2"], ("newc", r * K, (r + 1) * K), A.max)
-        ts("ix" + n, W["idx"], W["t3"], col_c, A.subtract, float(L * (r + 1)), A.add)
-        ts("sn" + n, ("sg", L + 1, ds * SEG, SEG), ("nc", 15, 16 * ds, 16), -1.0, A.mult)
+        scan("nc" + n, W["nc"], W["ir"], W["ne"], 0.0, A.min, A.add)
+        scan("t3" + n, W["t3"], W["pp"], ("newc", 2 * r * K, 2 * (r + 1) * K), 0.0, A.add, A.min)
+        ts("ix" + n, W["idx"], ("t3", 1, 2 * K, 2), ("cols", 4 + r, 5 + r), A.add, -1.0, A.mult)
+        act("sn" + n, ("sg", L + 1 + SEG, (ds + 1) * SEG, SEG), ("nc", 15, 16 * ds, 16), F.Copy, scale=-1.0)
         quant("qh" + n, (hq, hp), W["h"])
 
         def hand_on(q):
@@ -263,26 +270,25 @@ def rank_program(g, core, T, topo):
         copy("nr" + n, "sv", W["nrow"], ("pt", NODES - L * (r + 1), NODES + have), W["idx"])
 
         for k in range(K):
-            own, cut, c = ("ff", 16 * k + 15, 16 * k + 16), 16 * k + 16, n + chr(97 + k)
+            cut, c = 16 * k + 16, n + chr(97 + k)
+            own = ("ff", cut - 1, cut)
             if k < ds:
-                j = k * SEG
+                j = (k + 1) * SEG
                 act("S" + c, ("sg", j, j + L), bank(SS), F.Sign, bias=own, scale=-1.0)
-                act("B" + c, ("sj", j, j + cut), ("sg", j, j + cut), F.Relu, accum_out=("acc", k, k + 1))
+                act("B" + c, ("sj", j - 1, j + cut), ("sg", j - 1, j + cut), F.Relu, accum_out=("acc", k, k + 1))
                 act("A" + c, ("sj", j + cut, j + L + 2), ("sg", j + cut, j + L + 2), F.Relu, scale=-1.0,
                     accum_out=("acc", K + k, K + k + 1))
             else:
-                j, o = (k - ds) * L, (k - ds) * M
+                j, o = (k - ds) * L, k * M
                 ts("E" + c, ("fl", j, j + cut), bank(SV, 0, cut), own, A.is_ge, 0.5, A.subtract)
                 if cut < L:
                     ts("G" + c, ("fl", j + cut, j + L), bank(SV, cut, L), own, A.is_gt, 0.5, A.subtract)
                 scan("C" + c, ("fs", o, o + M), ("fl", j, j + M), ("fl", j + M, j + L), ("nc", cut - 1, cut), A.add, A.add)
 
         order = ("pt", NODES + have + L, NODES + have + 2 * L)
-        ts("rv" + n, ("rv", 0, K - ds), ("fs", M - 1, (K - ds) * M, M), M - 16.0, A.add)
-        scatter("sv" + n, order, ("rv", 0, K - ds), ("nrow", 16 * ds, L))
-        tt("c1" + n, ("c1", 0, ds), ("acc", K, K + ds), ("acc", 0, ds), A.subtract)
-        copy("rs" + n, "v", ("rs", 0, ds), ("c1", 0, ds))
-        scatter("ss" + n, order, ("rs", 0, ds), ("nrow", 0, 16 * ds))
+        tt("c1" + n, ("fs", M - 1, ds * M, M), ("acc", K, K + ds), ("acc", 0, ds), A.subtract)
+        ts("rs" + n, W["rv"], ("fs", M - 1, K * M, M), M - 16.0, A.add)
+        scatter("ss" + n, order, W["rv"], W["nrow"])
         for b in range(4):
             mm("md%d%d" % (r, b), DEC[b], side("e", b), (lq, lp))
         for b in range(4):
@@ -300,11 +306,11 @@ def rank_program(g, core, T, topo):
         one_round(r)
 
     reading(R)
-    dma("oc", "y", "dout", T.oc[:], u8(qz[0]), [], [qz[0]])
     for k in range(4):
         dma("os%d" % k, "ys", "dout", T.osc[4 * k:4 * k + 4, :], T.zp[32 * k:32 * k + 4, :], [], [qz[1]])
     for i in range(2):
         half = ("ys", i * M, (i + 1) * M)
+        dma("oc%d" % i, "ys", "dout", T.oc[:, 4 * M * i:4 * M * (i + 1)], u8(side("z", i, M)[0]), [], [side("z", i, M)[0]])
         mm("my%d" % i, i, qu, side("z", i, M))
         copy("y%d" % i, ("vs", "sv")[i], half, bank(i, 0, M))
         dma("oy%d" % i, ("ys", "sy")[i], "dout", T.y[:, i * M:(i + 1) * M], ap(half), [], [half])

@@ -5,34 +5,48 @@ NODES = C + L * R
 HELD = C + L * (R - 1)
 K = L // 16
 M = L // 2
-DSS = (7, 7, 7)
-ZH = (1, 2, 2, 2)
-ORDER = "lx ip lt one ii lp pb ce pm cum iu cm cc sm in eb ar mk sk uo qe1 tu ay x15 cr qe0 qe2 pt qe3 p40 p41 ca pl1 pl0 pl2 lu pu lw p42 p43 vt0 t20 ls ax a01 vt1 pl3 pp vt2 z000 n0 vt3 z002.s qu z003 z001 uq up qz00 a03 nw a00.v mv0 a02 ml00 bm00 ml01 bm01 h00 ml02 ff00 ml03 h01 ff01 ms0 G0i h02 ne0 h03 E0h G0r nc0 t00 S0d G0l G0q qh0 S0b G0j S0c G0h go0 sn0 E0s S0e G0s S0g C0h E0j E0o B0c S0a G0k E0k t10 A0b E0i E0m A0g E0n A0e G0o G0n S0f G0p E0r A0d C0n G0m A0f C0k C0i B0b E0p B0e B0d E0q A0a C0s B0a E0l A0c C0q t30 B0f E0t B0g n1 C0p ix0 C0r C0o C0t nr0 C0l C0m C0j c10 rs0 ss0 md03 md00 md02 d03 md01 w00 d02 xx01 d01 xx00 to01 w02 d00 to00 z110 w03 z100 w01 z112.s z113 z111 z101.v z102.s z103 a13 qz11 qz10 a10.v t21 a11 mv1 ml10 ml12 bm11 bm10 ml11 h10 ff11 ml13 ff10 h12 ms1 E1k h11 G1i G1s G1k t01 h13 ne1 S1e E1h G1j S1d nc1 qh1 S1a E1t sn1 S1b go1 E1i B1a E1q A1d E1j t11 B1b S1g E1l G1h S1f E1m A1a G1r E1o G1p S1c E1p A1e G1l E1n A1c t31 C1i G1m A1f G1q C1p E1s A1g B1f G1o B1c C1j B1g C1s C1k B1e C1h md11 B1d ix1 C1m A1b md13 C1l E1r md12 nr1 md10 G1n C1q C1r d12 C1o C1t C1n c11 d10 w13 a12 rs1 w11 ss1 d13 d11 w10 xx10 xx11 to10 w12 t22 z200 to11 z203 z210 z211.v z213.s z212 z201 z202 a21 qz21 qz20 a20.v a22 mv2 ml21 ml20 bm21 bm20 ml22 h21 ff21 ms2 ff20 h20 ml23 E2p h22 ne2 S2g E2h E2q S2c E2l h23 E2t S2a G2p G2j S2e G2o nc2 qh2 S2b E2j sn2 S2f G2h go2 B2a E2i A2a G2l C2p B2c G2r E2r t02 B2g B2b G2q t12 A2g E2m C2l S2d E2n B2f G2i A2f G2m t32 G2n B2e G2s B2d E2s A2e E2o A2d G2k A2c C2n C2h C2o A2b C2i E2k C2t C2s md20 ix2 C2r C2q md22 C2k nr2 C2m md21 C2j c12 md23 w20 a23 rs2 w22 ss2 w21 ol xx21 xx20 to21 w23 z310 z312 z311 to20 z313 z303.s z302 z301 qz31 z300.v oc1.s my1 qz30 y1 my0 oc0 os2.s os0 oy1 y0 os3 oy0 os1"
-DS, DV = max(DSS), K - min(DSS)
-SEG = L + 8
+MORE = (1, 2, 1)
+ORDER = "pb lx lt ip lp ii pm ph cc ch cm iu x15 in f13 mk f03.g uo l0 ca g0 f12 t20 ar tu f02 cr f00 l2.s ci f01.s pu f10 ih nw nz uf g1.s ay lu pl3.v pl0.s ls lw pl2.v n0 ax l1 vt3 pl1 f11.g vt2 z013.s ie z003.s vt1 z012 z002 vt0 cum z001 z011 qu z000.v z010 gw uq up qz01 a02 qz00 n1 eb mh01 mh00 a00 ml02 bm01 ml01 qe3 ml00 bm00 h02 ms0 ff01 ml03 qe1 h01 ff00 mv0 E0o E0s h00 E0n G0s G0q E0m G0p G0m t00 S0c G0j S0t G0r E0p h03 E0r dg01 G0i A0t G0o S0a G0f qh0 S0b G0d A0c G0e A0a G0h go0 R06 E0q S0l G0g A0b dg00 R05 R01 S0k R03 R04 t10 G0n A0l cs00 A0k mh t30 cs01 pp R02 R07 ix0 df00 df01 a01 nc0 qe0 ra0 N0 T0 nr0 xs0 rb0 U01 U00 xr0 pt xy0 md03 rv0 qe2 a03 md00 ss0 md01 md02 d00 d01 w03 d02 xx00 w00 d03 to00 xx01 w01 z100 to01 w02 z103.s z110.v z101 z113 z102 z112.v z111 qz10 t21 a11 qz11 mh10 a12 go1 mh11 bm10 ms1 mv1 ff10 bm11 dg10 S1c S1a ff11 G1d S1j G1f S1b E1p E1m E1n G1p G1r G1s E1q S1t G1o A1c G1q G1i S1l E1o G1h A1t E1r A1b G1e G1n G1m S1k R15 A1a G1g ml11 E1s R13 ml13 A1l R11 dg11 A1k ml12 cs10 A1j ml10 t01 h11 cs11 h12 t11 h10 R16 R14 df10 h13 df11 R12 R17 nc1 a10 t31 T1 ra1 N1 ix1 xs1 rb1 U10 U11 nr1 xr1 qh1 xy1 a13 md12 rv1 md13 ss1 md11 d12 md10 w11 xx11 xx10 d11 to11 w13 t22 z211 to10 w10 z201 w12 z210.v z200 z212.v z213.s z202.v z203.s qz21 d10 qz20 d13 mh21 a21 go2 mh20 bm21 ms2 mv2 bm20 a23 ff21 ff20 E2n E2s S2t G2q G2s G2r S2l dg21 S2k E2r S2b G2d G2m E2q t02 A2t G2f S2a dg20 G2p E2p t12 E2o A2b E2m G2o G2g G2j S2c G2i A2a G2h ml23 G2n A2c G2e ml20 R26 A2k R25 ml22 R24 A2l R23 ml21 cs20 h23 h20 cs21 h21 R22 a20 df20 R21 R27 df21 t32 nc2 ra2 N2 h22 T2 rb2 ix2 xs2 U21 U20 nr2 xr2 qh2 xy2 a22 md20 rv2 md22 ss2 md21 md23 w21 ol xx21 w23 to21 xx20 w20 z313.s to20 w22 z311 z303 z310 z312.v z302 z300.v z301 qz31 my1 oc1 qz30 y1.v os3 os2.s my0 os1 y0.s oc0.s oy1 os0.s oy0"
 BIG = 2.0 ** 93
 HOLD = 2048.0
 DROP = 2.0 ** 22
+LIFT = 1000.0
 BANK = 512
+GAP = 360
 CODES = "float8_e4m3fn_x4"
+SLOTS, PAD = 6, 8
+Q = (K - 2) // 2
+RUN = 8 * (K - 2)
 
 WIDTHS = {
-    "bfloat16": {"xs": 4 * C, "us": 512, "ones": 520, "eb": 520, "ir": L, "pool": 4 * HELD, "vt": 4 * NODES, "at": 4 * L,
-                 "z": 4 * L, "h": 4 * L, "ne": L, "nc": L, "fl": DV * L, "fs": K * M, "sg": (DS + 1) * SEG, "sj": (DS + 1) * SEG},
-    "float32": {"mk": L, "ar": L, "ax": L, "cols": 8, "newc": 2 * R * K, "pp": 2 * K, "x15": K, "pt": 2 * NODES + L,
-                "bm": L, "ff": L, "t0": K, "t3": 2 * K, "nrow": L, "acc": 2 * K, "xx": L, "ys": L},
-    "int32": {"pari": C // 16, "topi": K, "ui": 12, "pi": 2, "pm": 2, "ni": R * K},
-    "uint16": {"uo": 8, "paru": C // 16, "par4": 4 * (C // 16), "topu": (R + 1) * K, "idx": K, "rv": K},
-    CODES: {"wq": 512, "uq": 128, "urq": 128, "eq": 512, "zq": L},
-    "uint8": {"wp": 512, "up": 128, "urp": 128, "ep": 512, "zp": L},
+    "bfloat16": {"xs": 4 * C, "us": 512, "eb": 520, "ir": L, "pool": 4 * HELD, "vt": 4 * NODES, "at": 4 * L,
+                 "z": 4 * L, "h": 4 * L, "fa": PAD + SLOTS * L, "fb": PAD + SLOTS * L, "sg": 13 * L,
+                 "gg": L + 32, "tt": 2 * L + 32, "mh": L + 32},
+    "float16": {"nc": M + 8, "uu": 6 * (L + 16), "pa": 2 * (PAD + SLOTS * M), "pr": (Q - 1) * RUN},
+    "float32": {"mk": L, "ar": L, "ax": L, "cols": 16, "newc": 2 * R * K, "pp": 2 * K, "x15": K, "pt": 2 * NODES + L,
+                "bm": L, "ff": L, "t0": K, "t3": 2 * K, "nrow": L, "rs": K, "xy": 3 * K, "xx": L, "ys": L, "lift": K},
+    "int32": {"pari": C // 16, "topi": K, "ui": 8, "pi": 2, "pm": 2, "ph": 2, "ni": R * K},
+    "uint16": {"uo": 8, "paru": C // 16, "topu": (R + 1) * K, "idx": K, "rv": K},
+    CODES: {"wq": 512, "vq": 512, "uq": 128, "urq": 128, "eq": 512, "hq": L, "gq": L, "z3q": L},
+    "uint8": {"wp": 512, "vp": 512, "up": 128, "urp": 128, "ep": 512, "hp": L, "gp": L, "z3p": L},
 }
 SCRATCH = {_n: ("sbuf", [128, _w], _d) for _d in WIDTHS for _n, _w in WIDTHS[_d].items()}
 SCRATCH["ps"] = ("psum", [128, 8 * BANK], "float32")
 for _t in range(R):
-    for _n, _d in (("hq", CODES), ("hp", "uint8"), ("lq", CODES), ("lp", "uint8")):
-        SCRATCH[_n + str(_t)] = ("sbuf", [128, L], _d)
+    for _n, _d in (("z%dq", CODES), ("z%dp", "uint8"), ("l%dq", CODES), ("l%dp", "uint8")):
+        SCRATCH[_n % _t] = ("sbuf", [128, L], _d)
 
-SEMAPHORES = ["cv", "cs", "ct", "cg", "dx", "du", "dpar", "dtop", "dwc", "dws", "dout", "sent"] + ["arr%d" % _t for _t in range(R)]
+SEMAPHORES = ["cv", "cs", "ct", "cg", "dx", "du", "dpar", "dtop", "dwc", "dws", "dout", "sent", "arrw"] + ["arr%d" % _t for _t in range(R)]
+
+
+def layer(k):
+    return k if k < 2 else (k - 2) % Q + 2 + ((k - 2) % Q > 0)
+
+
+def spans(k):
+    if k < 2 + Q:
+        return [(k + 1, K if k < 2 else k + 1 + Q, True)]
+    return [s for s in ((k + 1, K, True), (2, k - Q, False)) if s[0] < s[1]]
 
 
 def rank_program(g, core, T, topo):
@@ -50,6 +64,7 @@ def rank_program(g, core, T, topo):
     total = {}
     known = {q: {} for q in queue}
     clock = {}
+    size = {}
     wrote, read, banks = {}, {}, {}
     steps = {}
 
@@ -65,6 +80,7 @@ def rank_program(g, core, T, topo):
 
     def issue(q, call, outs, ins, sem):
         held = [r[1] // BANK for r in ins + outs if r[0] == "ps"]
+        narrow = q == "v" and all(SCRATCH[r[0]][2].endswith("t16") for r in ins + outs)
         outs, ins = [r for r in outs if r[0] != "ps"], [r for r in ins if r[0] != "ps"]
         need = {}
         for b in held:
@@ -81,15 +97,23 @@ def rank_program(g, core, T, topo):
             for sb in list(need):
                 if sa != sb and sa in need and sb in need and clock[(sb, need[sb])].get(sa, 0) >= need[sa]:
                     del need[sa]
+        own = "c" + q
+        if known[q].get(own, 0) < need.get(own, 0):
+            v, since = total[own], 0
+            while v > need[own] and since < GAP:
+                since += size[(own, v)]
+                v -= 1
+            need[own] = v
         for s in sorted(need, key=lambda s: -need[s]):
             if known[q].get(s, 0) < need[s]:
                 queue[q].wait_ge(T.sem[s], need[s])
                 learn(known[q], clock[(s, need[s])])
         far = sem is not None and sem.startswith("arr")
         step = 1 if sem is None else 2 * lanes if far else 16
-        sem = sem or "c" + q
+        sem = sem or own
         total[sem] = total.get(sem, 0) + step
         mark = (sem, total[sem])
+        size[mark] = max(16, len(range(*outs[0][1:])) // (2 if narrow else 1)) if outs else 0
         clock[mark] = dict(clock.get((sem, total[sem] - step), {}))
         if far:
             call(q)
@@ -118,8 +142,16 @@ def rank_program(g, core, T, topo):
     def u32(r):
         return ap(r).bitcast(dt.uint32)
 
-    def memset(name, out, c):
-        step(name, "v", lambda q: V.memset(ap(out), c), [out], [])
+    def fill(name, qs, out, c):
+        n = len(range(*out[1:]))
+
+        def call(q):
+            if q == "v":
+                return V.memset(ap(out), c)
+            if q == "s":
+                return S.activation(ap(out), T.ir[:, 0:n], F.Identity, bias=c, scale=0.0)
+            return g.iota(ap(out), [[0, n]], int(c), 0, allow_small_or_imprecise_dtypes=True)
+        step(name, qs, call, [out], [("ir", 0, n)] if "s" in qs else [])
 
     def ts(name, out, in0, s1, op0, s2=None, op1=None):
         ops = [op0] if op1 is None else [op0, op1]
@@ -131,6 +163,9 @@ def rank_program(g, core, T, topo):
 
     def scan(name, out, d0, d1, init, op0, op1):
         step(name, "v", lambda q: V.tensor_tensor_scan(ap(out), ap(d0), ap(d1), ap(init), op0, op1), [out], [d0, d1, init])
+
+    def turn(name, out, in_):
+        step(name, "v", lambda q: V.transpose(ap(out), ap(in_)), [out], [in_])
 
     def copy(name, qs, out, in_, off=None):
         def call(q):
@@ -163,6 +198,12 @@ def rank_program(g, core, T, topo):
     def dma(name, qs, sem, dst, src, outs, ins):
         step(name, qs, lambda q: queue[q].dma_start(dst, src), outs, ins, sem)
 
+    def hand(name, sem, to, frm):
+        def call(q):
+            g.remote_dma(u8(to[0]), u8(frm[0]), T.sem[sem], T.sem.sent, pid, rid, wide)
+            g.remote_dma(ap(to[1]), ap(frm[1]), T.sem[sem], T.sem.sent, pid, rid, wide)
+        step(name, "g", call, to, frm, sem)
+
     def plane(name, t, a, b):
         w = SCRATCH[name][1][1] // 4
         return (name, t * w + a, t * w + b)
@@ -170,13 +211,16 @@ def rank_program(g, core, T, topo):
     def side(name, b=0, n=128):
         return (name + "q", n * b, n * b + n), (name + "p", n * b, n * b + n)
 
-    PC = C // 16
+    def cells(y, a, e, hop=1):
+        return ("fa", "fb")[y % 2], PAD + SLOTS * a + y // 2, PAD + SLOTS * e, SLOTS * hop
+
     W = {n: (n, 0, SCRATCH[n][1][1]) for n in SCRATCH}
     loose = {"allow_small_or_imprecise_dtypes": True}
-    col_c, col_a, col_e, col_m = (("cols", i, i + 1) for i in range(4))
-    pm, pi = ("pm", 0, 1), ("pi", 0, 1)
-    qz, qu, qur = side("z", 0, L), side("u"), side("ur")
-    SV, SS, LAY, DEC = 0, 1, (2, 3, 4, 5), (6, 7, 2, 3)
+    col_c, col_a, col_h, col_m = (("cols", i, i + 1) for i in range(4))
+    col_i = ("cols", 8, 9)
+    pm, pi, ph = ("pm", 0, 1), ("pi", 0, 1), ("ph", 0, 1)
+    qu, qur = side("u"), side("ur")
+    SV, SS, LAY, HALF = 0, 1, (2, 3, 4, 5), (6, 7)
 
     dma("lx", "y", "dx", T.xs[:], T.x[:], [W["xs"]], [])
     dma("lp", "s", "dpar", T.pari[:], T.par[:], [W["pari"]], [])
@@ -187,29 +231,40 @@ def rank_program(g, core, T, topo):
 
     iota("ip", pi, [[0, 1]], 0, 1)
     iota("ii", W["ir"], [[0, K], [1, 16]], 0, **loose)
-    iota("iu", W["ui"], [[16, 12]], 0)
+    iota("ie", W["eb"], [[1, 520]], -3, -4, **loose)
+    iota("iu", W["ui"], [[16, 8]], 0)
     iota("in", W["ni"], [[-L, R], [16, K]], -L)
-    memset("one", W["ones"], 1.0)
+    iota("cum", ("pt", 0, C), [[1, C]], 0, **loose)
+    iota("ih", W["mh"], [[0, K // 2 + 1], [1, 2], [0, 16]], 0, **loose)
     ts("pm", pm, pi, 15, A.bitwise_and)
-    scan("cum", ("pt", 0, 520), W["ones"], W["ones"], -1.0, A.add, A.mult)
-    ts("ce", col_e, pi, 4.0, A.mult, 3.0, A.add)
+    ts("ph", ph, pi, 4, A.logical_shift_right, 1, A.bitwise_and)
+    ts("ch", col_h, ph, 1.0, A.subtract)
     ts("cm", col_m, pm, -BIG, A.mult)
-    ts("eb", W["eb"], ("pt", 0, 520), col_e, A.is_equal)
+    ts("eb", W["eb"], W["eb"], 0.0, A.is_equal)
+    act("ci", col_i, col_m, F.Copy, scale=-1.0 / BIG)
+    act("mh", W["mh"], W["mh"], F.Abs, bias=col_h)
     act("mk", W["mk"], W["ir"], F.Abs, bias=col_m, scale=BIG)
-    act("ar", W["ar"], W["ir"], F.Identity, bias=-3.0e28, scale=6.0e28)
+    act("ar", W["ar"], W["ir"], F.Identity, bias=3.0e28, scale=-6.0e28)
+    idle = PAD + 16 * (2 + Q) * SLOTS
+    for i, b in enumerate(("fa", "fb")):
+        for j in range(4):
+            fill("f%d%d" % (i, j), "vsg", (b, j * idle // 4, (j + 1) * idle // 4), 1.0)
+    fill("g0", "vsg", ("gg", 0, 16), 0.0)
+    fill("g1", "vsg", ("gg", L + 16, L + 32), 0.0)
+    ts("uf", ("uu", 45, 6 * (L + 16), 16), ("ir", 0, 124), 0.0, A.mult, LIFT, A.add)
+    ts("nz", ("nc", 7, 8), ("ir", 0, 1), 0.0, A.mult)
+    fill("l0", "vs", W["lift"], LIFT)
+    fill("l1", "vs", ("lift", 2, K - 1 - Q), LIFT - 16)
+    fill("l2", "vs", ("lift", K - 1, K), LIFT + 16 * (Q - 1))
     for b in range(4):
         quant("qe%d" % b, side("e", b), ("eb", 3 - b, 515 - b))
     ts("cc", col_c, pm, 15.0, A.subtract, -HOLD, A.mult)
     ts("ca", col_a, pm, 1.0 - HOLD, A.mult, 15.0 * HOLD, A.add)
-    copy("uo", "v", W["uo"], ("ui", 0, 8))
-    ts("sk", ("sg", L + SEG, (DS + 1) * SEG, SEG), ("ui", 0, DS), -1.0, A.mult)
-    memset("sm", ("sg", SEG - 1, (DS + 1) * SEG, SEG), M - 16.0)
+    copy("uo", "v", W["uo"], W["ui"])
     ts("nw", ("newc", 1, 2 * R * K, 2), W["ni"], col_a, A.add, -1.0, A.mult)
-    memset("pb", ("pp", 0, 2 * K, 2), BIG)
+    fill("pb", "v", ("pp", 0, 2 * K, 2), BIG)
     ts("cr", ("cols", 4, 4 + R), ("ni", 0, R * K, K), col_c, A.add)
     copy("pu", "v", W["paru"], W["pari"])
-    for t in range(4):
-        ts("p4%d" % t, ("par4", t * PC, (t + 1) * PC), W["pari"], 4.0, A.mult, float(t), A.add)
     copy("tu", "v", ("topu", 0, K), W["topi"])
     ts("x15", W["x15"], W["topi"], col_c, A.add)
     copy("pp", "sv", ("pt", NODES, NODES + C), ("pt", 0, C), W["paru"])
@@ -220,81 +275,102 @@ def rank_program(g, core, T, topo):
 
     for t in range(4):
         copy("pl%d" % t, ("vsg", "svg", "gsv", "gsv")[t], plane("pool", t, 0, C), ("xs", t, 4 * C, 4))
-    for t in range(4):
-        tt("vt%d" % t, plane("vt", t, 0, C), W["xs"], plane("pool", t, 0, C), A.add, ("par4", t * PC, (t + 1) * PC))
+        tt("vt%d" % t, plane("vt", t, 0, C), plane("pool", t, 0, C), ("xs", t, 4 * C, 4), A.add, W["paru"])
     quant("qu", qu, W["us"])
     step("uq", "v", lambda q: V.tensor_copy(u32(qur[0]), u32(qu[0]).indirect(T.uo[:])), [qur[0]], [qu[0], W["uo"]])
     copy("up", "sv", qur[1], qu[1], W["uo"])
     iota("n1", ("pt", C, NODES - L), [[-L, R - 1], [1, L]], NODES - L, **loose)
 
     def reading(r):
-        n = L // ZH[r]
-        for i in range(ZH[r]):
+        for i in range(2):
             for t in range(4):
-                copy("z%d%d%d" % (r, i, t), "vs" if t > 1 else "sv", ("z", 4 * n * i + t, 4 * n * (i + 1), 4),
-                     plane("vt", t, 0, C + L * r), ("topu", r * K + i * n // 16, r * K + (i + 1) * n // 16))
-            quant("qz%d%d" % (r, i), side("z", i, n), ("z", 4 * n * i, 4 * n * (i + 1)))
+                copy("z%d%d%d" % (r, i, t), "vs" if t > 2 else "sv", ("z", 4 * M * i + t, 4 * M * (i + 1), 4),
+                     plane("vt", t, 0, C + L * r), ("topu", r * K + i * K // 2, r * K + (i + 1) * K // 2))
+            quant("qz%d%d" % (r, i), side("z%d" % r, i, M), ("z", 4 * M * i, 4 * M * (i + 1)))
 
     def one_round(r):
-        have, ds, n = C + L * r, DSS[r], str(r)
+        have, n = C + L * r, str(r)
+        mine = 2 + Q - MORE[r]
         held = W["x15"] if r == 0 else ("xx", 15, L, 16)
-        hq, hp, lq, lp = (W[b + n] for b in ("hq", "hp", "lq", "lp"))
+        qz, came = side("z" + n, 0, L), side("l" + n, 0, L)
+        qh = side("h" if r else "g", 0, L)
         reading(r)
+        if r:
+            hand("go" + n, "arr" + n, came, qz)
         for t in range(4):
             copy("a%d%d" % (r, t), "sv", plane("at", t, 0, L), plane("pool", t, 0, have), ("topu", r * K, (r + 1) * K))
+        for i in range(2):
+            mm("mh%d%d" % (r, i), HALF[i], qur, side("z" + n, i, M))
         mm("mv" + n, SV, qur, qz)
         mm("ms" + n, SS, qur, qz)
-        for b in range(4):
-            mm("ml%d%d" % (r, b), LAY[b], side("w", b), qz)
-            act("h%d%d" % (r, b), ("h", b, 4 * L, 4), bank(LAY[b]), F.Relu, scale=0.015625)
 
         for i in range(2):
             a, e = i * M, (i + 1) * M
-            tt("bm%d%d" % (r, i), ("bm", a, e), bank(SV, a, e), ("mk", a, e), A.subtract)
-            scan("ff%d%d" % (r, i), ("ff", a, e), ("ar", a, e), ("bm", a, e), 0.0, A.min, A.max)
+            tt("bm%d%d" % (r, i), ("bm", a, e), bank(HALF[i], 0, M), ("mk", a, e), A.add)
+            scan("ff%d%d" % (r, i), ("ff", a, e), ("ar", a, e), ("bm", a, e), 0.0, A.max, A.min)
 
         act("t0" + n, W["t0"], ("ff", 15, L, 16), F.Sign, bias=2.0 ** -124)
         act("t1" + n, ("pp", 1, 2 * K, 2), W["t0"], F.Relu, scale=BIG)
         act("t2" + n, ("newc", 2 * r * K, 2 * (r + 1) * K, 2), held, F.Copy, scale=-1.0)
-        tt("ne" + n, W["ne"], bank(SV), W["ff"], A.not_equal)
-        scan("nc" + n, W["nc"], W["ir"], W["ne"], 0.0, A.min, A.add)
         scan("t3" + n, W["t3"], W["pp"], ("newc", 2 * r * K, 2 * (r + 1) * K), 0.0, A.add, A.min)
         ts("ix" + n, W["idx"], ("t3", 1, 2 * K, 2), ("cols", 4 + r, 5 + r), A.add, -1.0, A.mult)
-        act("sn" + n, ("sg", L + 1 + SEG, (ds + 1) * SEG, SEG), ("nc", 15, 16 * ds, 16), F.Copy, scale=-1.0)
-        quant("qh" + n, (hq, hp), W["h"])
-
-        def hand_on(q):
-            g.remote_dma(u8(lq), u8(hq), T.sem["arr" + n], T.sem.sent, pid, rid, wide)
-            g.remote_dma(ap(lp), ap(hp), T.sem["arr" + n], T.sem.sent, pid, rid, wide)
-        step("go" + n, "g", hand_on, [lq, lp], [hq, hp], "arr" + n)
         copy("nr" + n, "sv", W["nrow"], ("pt", NODES - L * (r + 1), NODES + have), W["idx"])
 
+        for i in range(2):
+            a, e = i * M, (i + 1) * M
+            tt("dg%d%d" % (r, i), cells(3, a, e), bank(HALF[i], 0, M), ("ff", a, e), A.is_gt)
+        scan("nc" + n, ("nc", 8, M + 8), cells(3, 0, L, 2), cells(3, 1, L, 2), 0.0, A.add, A.add)
         for k in range(K):
-            cut, c = 16 * k + 16, n + chr(97 + k)
-            own = ("ff", cut - 1, cut)
-            if k < ds:
-                j = (k + 1) * SEG
-                act("S" + c, ("sg", j, j + L), bank(SS), F.Sign, bias=own, scale=-1.0)
-                act("B" + c, ("sj", j - 1, j + cut), ("sg", j - 1, j + cut), F.Relu, accum_out=("acc", k, k + 1))
-                act("A" + c, ("sj", j + cut, j + L + 2), ("sg", j + cut, j + L + 2), F.Relu, scale=-1.0,
-                    accum_out=("acc", K + k, K + k + 1))
-            else:
-                j, o = (k - ds) * L, k * M
-                ts("E" + c, ("fl", j, j + cut), bank(SV, 0, cut), own, A.is_ge, 0.5, A.subtract)
-                if cut < L:
-                    ts("G" + c, ("fl", j + cut, j + L), bank(SV, cut, L), own, A.is_gt, 0.5, A.subtract)
-                scan("C" + c, ("fs", o, o + M), ("fl", j, j + M), ("fl", j + M, j + L), ("nc", cut - 1, cut), A.add, A.add)
+            own, c = ("ff", 16 * k + 15, 16 * k + 16), n + chr(97 + k)
+            for a, e, later in spans(k):
+                a, e = 16 * a, 16 * e
+                if 3 <= k < mine or 2 + Q < k < K - 1:
+                    row = bank(SV, a, e) if a < M < e else bank(HALF[a // M], a % M, a % M + e - a)
+                    ts("EG"[later] + c, cells(layer(k), a, e), row, own, A.is_gt if later else A.is_ge)
+                else:
+                    sg = ("sg", min(k, 12) * L + a, min(k, 12) * L + e)
+                    act("S" + c, sg, bank(SS, a, e), F.Sign if later else F.Relu, bias=own, scale=-1.0)
+                    act("A" + c, cells(layer(k), a, e), sg, F.Relu if later else F.Sign, scale=-1.0, accum_out=("rs", k, k + 1))
+
+        for q in range(1, Q - 1):
+            scan("R%d%d" % (r, q), ("pr", (q - 1) * RUN, q * RUN), cells(q + 3, 32, L, 2), cells(q + 3, 33, L, 2),
+                 -16.0, A.add, A.add)
+        end, e = (mine - 3) * (RUN + 8), 3 * (L + 31)
+        tt("ra" + n, ("rs", 3, mine), ("pr", 8 * Q + 15, end, RUN + 8), ("pr", 15, end, RUN + 8), A.subtract)
+        tt("rb" + n, ("rs", 3 + Q, K - 1), ("pr", RUN - 1, (Q - 2) * RUN, RUN), ("rs", 3, 1 + Q), A.subtract)
+        tt("xr" + n, ("uu", e + 16, e + 3 * L, 48), W["rs"], ("nc", 15, M + 8, 8), A.add)
+        tt("xs" + n, ("uu", e + 32, e + 3 * L, 48), W["lift"], ("nc", 7, M, 8), A.subtract)
+
+        for i in range(2):
+            a, o = PAD + SLOTS * M * i, (PAD + SLOTS * M) * i + PAD
+            scan("cs%d%d" % (r, i), ("pa", o - 1, o + SLOTS * M), ("fa", a - 1, a + SLOTS * M), ("fb", a - 1, a + SLOTS * M),
+                 0.0, A.add, A.add)
+            scan("df%d%d" % (r, i), ("gg", 16 + M * i, 16 + M * (i + 1)), ("pa", o - 1, o + SLOTS * M - 1, SLOTS),
+                 ("pa", o + SLOTS - 1, o + SLOTS * M, SLOTS), 0.0, A.max, A.subtract)
+        for i, (a, b) in enumerate(((16, L + 16), (0, L + 32))):
+            to = ("tt", i * L, i * L + b - a)
+            turn("TN"[i] + n, to, ("gg", a, b))
+            scan("U%d%d" % (r, i), ("uu", 3 * to[1], 3 * to[2], 3), to, ("mh", 0, b - a), 0.0, A.add, A.mult)
 
         order = ("pt", NODES + have + L, NODES + have + 2 * L)
-        tt("c1" + n, ("fs", M - 1, ds * M, M), ("acc", K, K + ds), ("acc", 0, ds), A.subtract)
-        ts("rs" + n, W["rv"], ("fs", M - 1, K * M, M), M - 16.0, A.add)
+        scan("xy" + n, W["xy"], ("uu", 45, 45 + 3 * L, 16), ("uu", e, e + 3 * L, 16), LIFT, A.min, A.add)
+        ts("rv" + n, W["rv"], ("xy", 2, 3 * K, 3), col_i, A.add, 16.0 * (2 * SLOTS - 1) - LIFT, A.add)
         scatter("ss" + n, order, W["rv"], W["nrow"])
+
         for b in range(4):
-            mm("md%d%d" % (r, b), DEC[b], side("e", b), (lq, lp))
+            mm("ml%d%d" % (r, b), LAY[b], side("v" if r else "w", b), came if r else qz)
+            act("h%d%d" % (r, b), ("h", b, 4 * L, 4), bank(LAY[b]), F.Relu, scale=0.015625)
+        quant("qh" + n, qh, W["h"])
+        if r == 0:
+            hand("go0", "arr0", came, qh)
+            hand("gw", "arrw", side("v", 0, 512), side("w", 0, 512))
+        for b in range(4):
+            mm("md%d%d" % (r, b), LAY[b], side("e", b), qh if r else came)
+
         for b in range(4):
             if r + 1 < R:
-                copy("d%d%d" % (r, b), "s", plane("pool", b, have, have + L), bank(DEC[b]))
-            tt("w%d%d" % (r, b), plane("vt", b, have, have + L), bank(DEC[b]), plane("at", b, 0, L), A.add)
+                copy("d%d%d" % (r, b), "sv", plane("pool", b, have, have + L), bank(LAY[b]))
+            tt("w%d%d" % (r, b), plane("vt", b, have, have + L), bank(LAY[b]), plane("at", b, 0, L), A.add)
         for i in range(2):
             a, e = i * M, (i + 1) * M
             scan("xx%d%d" % (r, i), ("xx", a, e), ("ax", a, e), ("pt", order[1] + a, order[1] + e), 0.0, A.add, A.max)
@@ -307,11 +383,11 @@ def rank_program(g, core, T, topo):
 
     reading(R)
     for k in range(4):
-        dma("os%d" % k, "ys", "dout", T.osc[4 * k:4 * k + 4, :], T.zp[32 * k:32 * k + 4, :], [], [qz[1]])
+        dma("os%d" % k, "ys", "dout", T.osc[4 * k:4 * k + 4, :], T.z3p[32 * k:32 * k + 4, :], [], [W["z3p"]])
     for i in range(2):
         half = ("ys", i * M, (i + 1) * M)
-        dma("oc%d" % i, "ys", "dout", T.oc[:, 4 * M * i:4 * M * (i + 1)], u8(side("z", i, M)[0]), [], [side("z", i, M)[0]])
-        mm("my%d" % i, i, qu, side("z", i, M))
+        dma("oc%d" % i, "ys", "dout", T.oc[:, 4 * M * i:4 * M * (i + 1)], u8(side("z3", i, M)[0]), [], [side("z3", i, M)[0]])
+        mm("my%d" % i, i, qu, side("z3", i, M))
         copy("y%d" % i, ("vs", "sv")[i], half, bank(i, 0, M))
         dma("oy%d" % i, ("ys", "sy")[i], "dout", T.y[:, i * M:(i + 1) * M], ap(half), [], [half])
 
@@ -321,6 +397,6 @@ def rank_program(g, core, T, topo):
         issue(q or qs[0], call, outs, ins, sem)
     assert not steps
 
-    g.wait_ge(T.sem.sent, 2 * lanes * R)
+    g.wait_ge(T.sem.sent, 2 * lanes * (R + 1))
     for sem in sorted(total):
         g.wait_ge(T.sem[sem], total[sem])

from concourse.mybir import dt, AluOpType, ActivationFunctionType

C, L, R = 384, 320, 3
NODES = C + L * R
HELD = C + L * (R - 1)
K = L // 16
M = L // 2
MORE = (1, 2, 1)
ORDER = "pb lx lt ip lp ii pm ph cc ch cm iu x15 in f13 mk f03.g uo l0 ca g0 f12 t20 ar tu f02 cr f00 l2.s ci f01.s pu f10 ih nw nz uf g1.s ay lu pl3.v pl0.s ls lw pl2.v n0 ax l1 vt3 pl1 f11.g vt2 z013.s ie z003.s vt1 z012 z002 vt0 cum z001 z011 qu z000.v z010 gw uq up qz01 a02 qz00 n1 eb mh01 mh00 a00 ml02 bm01 ml01 qe3 ml00 bm00 h02 ms0 ff01 ml03 qe1 h01 ff00 mv0 E0o E0s h00 E0n G0s G0q E0m G0p G0m t00 S0c G0j S0t G0r E0p h03 E0r dg01 G0i A0t G0o S0a G0f qh0 S0b G0d A0c G0e A0a G0h go0 R06 E0q S0l G0g A0b dg00 R05 R01 S0k R03 R04 t10 G0n A0l cs00 A0k mh t30 cs01 pp R02 R07 ix0 df00 df01 a01 nc0 qe0 ra0 N0 T0 nr0 xs0 rb0 U01 U00 xr0 pt xy0 md03 rv0 qe2 a03 md00 ss0 md01 md02 d00 d01 w03 d02 xx00 w00 d03 to00 xx01 w01 z100 to01 w02 z103.s z110.v z101 z113 z102 z112.v z111 qz10 t21 a11 qz11 mh10 a12 go1 mh11 bm10 ms1 mv1 ff10 bm11 dg10 S1c S1a ff11 G1d S1j G1f S1b E1p E1m E1n G1p G1r G1s E1q S1t G1o A1c G1q G1i S1l E1o G1h A1t E1r A1b G1e G1n G1m S1k R15 A1a G1g ml11 E1s R13 ml13 A1l R11 dg11 A1k ml12 cs10 A1j ml10 t01 h11 cs11 h12 t11 h10 R16 R14 df10 h13 df11 R12 R17 nc1 a10 t31 T1 ra1 N1 ix1 xs1 rb1 U10 U11 nr1 xr1 qh1 xy1 a13 md12 rv1 md13 ss1 md11 d12 md10 w11 xx11 xx10 d11 to11 w13 t22 z211 to10 w10 z201 w12 z210.v z200 z212.v z213.s z202.v z203.s qz21 d10 qz20 d13 mh21 a21 go2 mh20 bm21 ms2 mv2 bm20 a23 ff21 ff20 E2n E2s S2t G2q G2s G2r S2l dg21 S2k E2r S2b G2d G2m E2q t02 A2t G2f S2a dg20 G2p E2p t12 E2o A2b E2m G2o G2g G2j S2c G2i A2a G2h ml23 G2n A2c G2e ml20 R26 A2k R25 ml22 R24 A2l R23 ml21 cs20 h23 h20 cs21 h21 R22 a20 df20 R21 R27 df21 t32 nc2 ra2 N2 h22 T2 rb2 ix2 xs2 U21 U20 nr2 xr2 qh2 xy2 a22 md20 rv2 md22 ss2 md21 md23 w21 ol xx21 w23 to21 xx20 w20 z313.s to20 w22 z311 z303 z310 z312.v z302 z300.v z301 qz31 my1 oc1 qz30 y1.v os3 os2.s my0 os1 y0.s oc0.s oy1 os0.s oy0"
BIG = 2.0 ** 93
HOLD = 2048.0
DROP = 2.0 ** 22
LIFT = 1000.0
BANK = 512
GAP = 360
CODES = "float8_e4m3fn_x4"
SLOTS, PAD = 6, 8
Q = (K - 2) // 2
RUN = 8 * (K - 2)

WIDTHS = {
    "bfloat16": {"xs": 4 * C, "us": 512, "eb": 520, "ir": L, "pool": 4 * HELD, "vt": 4 * NODES, "at": 4 * L,
                 "z": 4 * L, "h": 4 * L, "fa": PAD + SLOTS * L, "fb": PAD + SLOTS * L, "sg": 13 * L,
                 "gg": L + 32, "tt": 2 * L + 32, "mh": L + 32},
    "float16": {"nc": M + 8, "uu": 6 * (L + 16), "pa": 2 * (PAD + SLOTS * M), "pr": (Q - 1) * RUN},
    "float32": {"mk": L, "ar": L, "ax": L, "cols": 16, "newc": 2 * R * K, "pp": 2 * K, "x15": K, "pt": 2 * NODES + L,
                "bm": L, "ff": L, "t0": K, "t3": 2 * K, "nrow": L, "rs": K, "xy": 3 * K, "xx": L, "ys": L, "lift": K},
    "int32": {"pari": C // 16, "topi": K, "ui": 8, "pi": 2, "pm": 2, "ph": 2, "ni": R * K},
    "uint16": {"uo": 8, "paru": C // 16, "topu": (R + 1) * K, "idx": K, "rv": K},
    CODES: {"wq": 512, "vq": 512, "uq": 128, "urq": 128, "eq": 512, "hq": L, "gq": L, "z3q": L},
    "uint8": {"wp": 512, "vp": 512, "up": 128, "urp": 128, "ep": 512, "hp": L, "gp": L, "z3p": L},
}
SCRATCH = {_n: ("sbuf", [128, _w], _d) for _d in WIDTHS for _n, _w in WIDTHS[_d].items()}
SCRATCH["ps"] = ("psum", [128, 8 * BANK], "float32")
for _t in range(R):
    for _n, _d in (("z%dq", CODES), ("z%dp", "uint8"), ("l%dq", CODES), ("l%dp", "uint8")):
        SCRATCH[_n % _t] = ("sbuf", [128, L], _d)

SEMAPHORES = ["cv", "cs", "ct", "cg", "dx", "du", "dpar", "dtop", "dwc", "dws", "dout", "sent", "arrw"] + ["arr%d" % _t for _t in range(R)]


def layer(k):
    return k if k < 2 else (k - 2) % Q + 2 + ((k - 2) % Q > 0)


def spans(k):
    if k < 2 + Q:
        return [(k + 1, K if k < 2 else k + 1 + Q, True)]
    return [s for s in ((k + 1, K, True), (2, k - Q, False)) if s[0] < s[1]]


def rank_program(g, core, T, topo):
    rank = T.rank_of(core)
    if rank is None:
        return
    nxt = T.cores[(rank + 1) % len(T.cores)]
    rid, pid = topo.addr(nxt)[0], topo.addr(nxt)[1]
    wide = topo.mask(core, nxt)
    lanes = len(topo.engines(core, nxt))
    A, F = AluOpType, ActivationFunctionType
    V, S = g.vector, g.scalar

    queue = {"v": V, "s": S, "t": g.tensor, "g": g, "y": g.sync}
    total = {}
    known = {q: {} for q in queue}
    clock = {}
    size = {}
    wrote, read, banks = {}, {}, {}
    steps = {}

    def ap(r):
        if not isinstance(r, tuple):
            return r
        return T[r[0]][:, r[1]:r[2]:r[3]] if len(r) > 3 else T[r[0]][:, r[1]:r[2]]

    def learn(into, frm):
        for s, v in frm.items():
            if into.get(s, 0) < v:
                into[s] = v

    def issue(q, call, outs, ins, sem):
        held = [r[1] // BANK for r in ins + outs if r[0] == "ps"]
        narrow = q == "v" and all(SCRATCH[r[0]][2].endswith("t16") for r in ins + outs)
        outs, ins = [r for r in outs if r[0] != "ps"], [r for r in ins if r[0] != "ps"]
        need = {}
        for b in held:
            learn(need, dict(mark for oq, mark in banks.get(b, {}).items() if oq != q))
        for r in ins + outs:
            w = wrote.get(r[0], {})
            for mark in {w[c] for c in range(*r[1:]) if c in w}:
                learn(need, dict([mark]))
        for r in outs:
            rd = read.get(r[0], {})
            for c in range(*r[1:]):
                learn(need, rd.get(c, {}))
        for sa in list(need):
            for sb in list(need):
                if sa != sb and sa in need and sb in need and clock[(sb, need[sb])].get(sa, 0) >= need[sa]:
                    del need[sa]
        own = "c" + q
        if known[q].get(own, 0) < need.get(own, 0):
            v, since = total[own], 0
            while v > need[own] and since < GAP:
                since += size[(own, v)]
                v -= 1
            need[own] = v
        for s in sorted(need, key=lambda s: -need[s]):
            if known[q].get(s, 0) < need[s]:
                queue[q].wait_ge(T.sem[s], need[s])
                learn(known[q], clock[(s, need[s])])
        far = sem is not None and sem.startswith("arr")
        step = 1 if sem is None else 2 * lanes if far else 16
        sem = sem or own
        total[sem] = total.get(sem, 0) + step
        mark = (sem, total[sem])
        size[mark] = max(16, len(range(*outs[0][1:])) // (2 if narrow else 1)) if outs else 0
        clock[mark] = dict(clock.get((sem, total[sem] - step), {}))
        if far:
            call(q)
        else:
            learn(clock[mark], known[q])
            call(q).then_inc(T.sem[sem], step)
        clock[mark][sem] = total[sem]
        for b in held:
            banks.setdefault(b, {})[q] = mark
        for r in ([] if far else ins):
            rd = read.setdefault(r[0], {})
            for c in range(*r[1:]):
                rd.setdefault(c, {})[sem] = total[sem]
        for r in outs:
            w, rd = wrote.setdefault(r[0], {}), read.setdefault(r[0], {})
            for c in range(*r[1:]):
                w[c] = mark
                rd.pop(c, None)

    def step(name, qs, call, outs, ins, sem=None):
        steps[name] = (qs, call, [r for r in outs if isinstance(r, tuple)], [r for r in ins if isinstance(r, tuple)], sem)

    def u8(r):
        return ap(r).bitcast(dt.uint8)

    def u32(r):
        return ap(r).bitcast(dt.uint32)

    def fill(name, qs, out, c):
        n = len(range(*out[1:]))

        def call(q):
            if q == "v":
                return V.memset(ap(out), c)
            if q == "s":
                return S.activation(ap(out), T.ir[:, 0:n], F.Identity, bias=c, scale=0.0)
            return g.iota(ap(out), [[0, n]], int(c), 0, allow_small_or_imprecise_dtypes=True)
        step(name, qs, call, [out], [("ir", 0, n)] if "s" in qs else [])

    def ts(name, out, in0, s1, op0, s2=None, op1=None):
        ops = [op0] if op1 is None else [op0, op1]
        step(name, "v", lambda q: V.tensor_scalar(ap(out), ap(in0), ap(s1), ap(s2), *ops), [out], [in0, s1, s2])

    def tt(name, out, in0, in1, op, off=None):
        step(name, "v", lambda q: V.tensor_tensor(ap(out), ap(in0).indirect(ap(off)) if off else ap(in0), ap(in1), op),
             [out], [in0, in1, off])

    def scan(name, out, d0, d1, init, op0, op1):
        step(name, "v", lambda q: V.tensor_tensor_scan(ap(out), ap(d0), ap(d1), ap(init), op0, op1), [out], [d0, d1, init])

    def turn(name, out, in_):
        step(name, "v", lambda q: V.transpose(ap(out), ap(in_)), [out], [in_])

    def copy(name, qs, out, in_, off=None):
        def call(q):
            src = ap(in_).indirect(ap(off)) if off else ap(in_)
            if q == "g":
                return g.affine_select(ap(out), src, [[0, out[2] - out[1]]], A.is_ge, 0.0, 0, 0)
            return V.tensor_copy(ap(out), src) if q == "v" else S.activation(ap(out), src, F.Copy)
        step(name, qs, call, [out], [in_, off])

    def scatter(name, win, off, in_):
        step(name, "v", lambda q: V.tensor_copy(ap(win).indirect(ap(off)), ap(in_)), [win], [off, in_])

    def act(name, out, in_, func, **kw):
        step(name, "s", lambda q: S.activation(ap(out), ap(in_), func, **{k: ap(kw[k]) for k in kw}),
             [out, kw.get("accum_out")], [in_, kw.get("bias")])

    def quant(name, to, in_):
        step(name, "v", lambda q: V.quantize_mx(ap(to[0]), ap(to[1]), ap(in_)), to, [in_])

    def bank(b, a=0, e=L):
        return ("ps", b * BANK + a, b * BANK + e)

    def mm(name, b, w, x):
        out = bank(b, 0, x[0][2] - x[0][1])
        step(name, "t", lambda q: g.tensor.matmul_mx(ap(out), ap(w[0]), ap(w[1]), ap(x[0]), ap(x[1]), True, True), [out], w + x)

    def iota(name, out, pattern, base, cm=0, **kw):
        step(name, "g", lambda q: g.iota(ap(out), pattern, base, cm, **kw), [out], [])

    def dma(name, qs, sem, dst, src, outs, ins):
        step(name, qs, lambda q: queue[q].dma_start(dst, src), outs, ins, sem)

    def hand(name, sem, to, frm):
        def call(q):
            g.remote_dma(u8(to[0]), u8(frm[0]), T.sem[sem], T.sem.sent, pid, rid, wide)
            g.remote_dma(ap(to[1]), ap(frm[1]), T.sem[sem], T.sem.sent, pid, rid, wide)
        step(name, "g", call, to, frm, sem)

    def plane(name, t, a, b):
        w = SCRATCH[name][1][1] // 4
        return (name, t * w + a, t * w + b)

    def side(name, b=0, n=128):
        return (name + "q", n * b, n * b + n), (name + "p", n * b, n * b + n)

    def cells(y, a, e, hop=1):
        return ("fa", "fb")[y % 2], PAD + SLOTS * a + y // 2, PAD + SLOTS * e, SLOTS * hop

    W = {n: (n, 0, SCRATCH[n][1][1]) for n in SCRATCH}
    loose = {"allow_small_or_imprecise_dtypes": True}
    col_c, col_a, col_h, col_m = (("cols", i, i + 1) for i in range(4))
    col_i = ("cols", 8, 9)
    pm, pi, ph = ("pm", 0, 1), ("pi", 0, 1), ("ph", 0, 1)
    qu, qur = side("u"), side("ur")
    SV, SS, LAY, HALF = 0, 1, (2, 3, 4, 5), (6, 7)

    dma("lx", "y", "dx", T.xs[:], T.x[:], [W["xs"]], [])
    dma("lp", "s", "dpar", T.pari[:], T.par[:], [W["pari"]], [])
    dma("lt", "s", "dtop", T.topi[:], T.top[:], [W["topi"]], [])
    dma("lu", "y", "du", T.us[:], T.u[:], [W["us"]], [("xs", 0, 1)])
    dma("lw", "y", "dwc", u8(W["wq"]), T.wc[:], [W["wq"]], [("xs", 0, 1)])
    dma("ls", "y", "dws", T.wp[:], T.ws[:], [W["wp"]], [("xs", 0, 1)])

    iota("ip", pi, [[0, 1]], 0, 1)
    iota("ii", W["ir"], [[0, K], [1, 16]], 0, **loose)
    iota("ie", W["eb"], [[1, 520]], -3, -4, **loose)
    iota("iu", W["ui"], [[16, 8]], 0)
    iota("in", W["ni"], [[-L, R], [16, K]], -L)
    iota("cum", ("pt", 0, C), [[1, C]], 0, **loose)
    iota("ih", W["mh"], [[0, K // 2 + 1], [1, 2], [0, 16]], 0, **loose)
    ts("pm", pm, pi, 15, A.bitwise_and)
    ts("ph", ph, pi, 4, A.logical_shift_right, 1, A.bitwise_and)
    ts("ch", col_h, ph, 1.0, A.subtract)
    ts("cm", col_m, pm, -BIG, A.mult)
    ts("eb", W["eb"], W["eb"], 0.0, A.is_equal)
    act("ci", col_i, col_m, F.Copy, scale=-1.0 / BIG)
    act("mh", W["mh"], W["mh"], F.Abs, bias=col_h)
    act("mk", W["mk"], W["ir"], F.Abs, bias=col_m, scale=BIG)
    act("ar", W["ar"], W["ir"], F.Identity, bias=3.0e28, scale=-6.0e28)
    idle = PAD + 16 * (2 + Q) * SLOTS
    for i, b in enumerate(("fa", "fb")):
        for j in range(4):
            fill("f%d%d" % (i, j), "vsg", (b, j * idle // 4, (j + 1) * idle // 4), 1.0)
    fill("g0", "vsg", ("gg", 0, 16), 0.0)
    fill("g1", "vsg", ("gg", L + 16, L + 32), 0.0)
    ts("uf", ("uu", 45, 6 * (L + 16), 16), ("ir", 0, 124), 0.0, A.mult, LIFT, A.add)
    ts("nz", ("nc", 7, 8), ("ir", 0, 1), 0.0, A.mult)
    fill("l0", "vs", W["lift"], LIFT)
    fill("l1", "vs", ("lift", 2, K - 1 - Q), LIFT - 16)
    fill("l2", "vs", ("lift", K - 1, K), LIFT + 16 * (Q - 1))
    for b in range(4):
        quant("qe%d" % b, side("e", b), ("eb", 3 - b, 515 - b))
    ts("cc", col_c, pm, 15.0, A.subtract, -HOLD, A.mult)
    ts("ca", col_a, pm, 1.0 - HOLD, A.mult, 15.0 * HOLD, A.add)
    copy("uo", "v", W["uo"], W["ui"])
    ts("nw", ("newc", 1, 2 * R * K, 2), W["ni"], col_a, A.add, -1.0, A.mult)
    fill("pb", "v", ("pp", 0, 2 * K, 2), BIG)
    ts("cr", ("cols", 4, 4 + R), ("ni", 0, R * K, K), col_c, A.add)
    copy("pu", "v", W["paru"], W["pari"])
    copy("tu", "v", ("topu", 0, K), W["topi"])
    ts("x15", W["x15"], W["topi"], col_c, A.add)
    copy("pp", "sv", ("pt", NODES, NODES + C), ("pt", 0, C), W["paru"])
    copy("pt", "sv", ("pt", NODES + C, NODES + C + L), ("pt", 0, C), ("topu", 0, K))
    iota("n0", ("pt", NODES - L, NODES), [[1, L]], C, **loose)
    act("ay", W["bm"], W["mk"], F.Sign)
    act("ax", W["ax"], W["bm"], F.Identity, bias=-DROP, scale=DROP + HOLD)

    for t in range(4):
        copy("pl%d" % t, ("vsg", "svg", "gsv", "gsv")[t], plane("pool", t, 0, C), ("xs", t, 4 * C, 4))
        tt("vt%d" % t, plane("vt", t, 0, C), plane("pool", t, 0, C), ("xs", t, 4 * C, 4), A.add, W["paru"])
    quant("qu", qu, W["us"])
    step("uq", "v", lambda q: V.tensor_copy(u32(qur[0]), u32(qu[0]).indirect(T.uo[:])), [qur[0]], [qu[0], W["uo"]])
    copy("up", "sv", qur[1], qu[1], W["uo"])
    iota("n1", ("pt", C, NODES - L), [[-L, R - 1], [1, L]], NODES - L, **loose)

    def reading(r):
        for i in range(2):
            for t in range(4):
                copy("z%d%d%d" % (r, i, t), "vs" if t > 2 else "sv", ("z", 4 * M * i + t, 4 * M * (i + 1), 4),
                     plane("vt", t, 0, C + L * r), ("topu", r * K + i * K // 2, r * K + (i + 1) * K // 2))
            quant("qz%d%d" % (r, i), side("z%d" % r, i, M), ("z", 4 * M * i, 4 * M * (i + 1)))

    def one_round(r):
        have, n = C + L * r, str(r)
        mine = 2 + Q - MORE[r]
        held = W["x15"] if r == 0 else ("xx", 15, L, 16)
        qz, came = side("z" + n, 0, L), side("l" + n, 0, L)
        qh = side("h" if r else "g", 0, L)
        reading(r)
        if r:
            hand("go" + n, "arr" + n, came, qz)
        for t in range(4):
            copy("a%d%d" % (r, t), "sv", plane("at", t, 0, L), plane("pool", t, 0, have), ("topu", r * K, (r + 1) * K))
        for i in range(2):
            mm("mh%d%d" % (r, i), HALF[i], qur, side("z" + n, i, M))
        mm("mv" + n, SV, qur, qz)
        mm("ms" + n, SS, qur, qz)

        for i in range(2):
            a, e = i * M, (i + 1) * M
            tt("bm%d%d" % (r, i), ("bm", a, e), bank(HALF[i], 0, M), ("mk", a, e), A.add)
            scan("ff%d%d" % (r, i), ("ff", a, e), ("ar", a, e), ("bm", a, e), 0.0, A.max, A.min)

        act("t0" + n, W["t0"], ("ff", 15, L, 16), F.Sign, bias=2.0 ** -124)
        act("t1" + n, ("pp", 1, 2 * K, 2), W["t0"], F.Relu, scale=BIG)
        act("t2" + n, ("newc", 2 * r * K, 2 * (r + 1) * K, 2), held, F.Copy, scale=-1.0)
        scan("t3" + n, W["t3"], W["pp"], ("newc", 2 * r * K, 2 * (r + 1) * K), 0.0, A.add, A.min)
        ts("ix" + n, W["idx"], ("t3", 1, 2 * K, 2), ("cols", 4 + r, 5 + r), A.add, -1.0, A.mult)
        copy("nr" + n, "sv", W["nrow"], ("pt", NODES - L * (r + 1), NODES + have), W["idx"])

        for i in range(2):
            a, e = i * M, (i + 1) * M
            tt("dg%d%d" % (r, i), cells(3, a, e), bank(HALF[i], 0, M), ("ff", a, e), A.is_gt)
        scan("nc" + n, ("nc", 8, M + 8), cells(3, 0, L, 2), cells(3, 1, L, 2), 0.0, A.add, A.add)
        for k in range(K):
            own, c = ("ff", 16 * k + 15, 16 * k + 16), n + chr(97 + k)
            for a, e, later in spans(k):
                a, e = 16 * a, 16 * e
                if 3 <= k < mine or 2 + Q < k < K - 1:
                    row = bank(SV, a, e) if a < M < e else bank(HALF[a // M], a % M, a % M + e - a)
                    ts("EG"[later] + c, cells(layer(k), a, e), row, own, A.is_gt if later else A.is_ge)
                else:
                    sg = ("sg", min(k, 12) * L + a, min(k, 12) * L + e)
                    act("S" + c, sg, bank(SS, a, e), F.Sign if later else F.Relu, bias=own, scale=-1.0)
                    act("A" + c, cells(layer(k), a, e), sg, F.Relu if later else F.Sign, scale=-1.0, accum_out=("rs", k, k + 1))

        for q in range(1, Q - 1):
            scan("R%d%d" % (r, q), ("pr", (q - 1) * RUN, q * RUN), cells(q + 3, 32, L, 2), cells(q + 3, 33, L, 2),
                 -16.0, A.add, A.add)
        end, e = (mine - 3) * (RUN + 8), 3 * (L + 31)
        tt("ra" + n, ("rs", 3, mine), ("pr", 8 * Q + 15, end, RUN + 8), ("pr", 15, end, RUN + 8), A.subtract)
        tt("rb" + n, ("rs", 3 + Q, K - 1), ("pr", RUN - 1, (Q - 2) * RUN, RUN), ("rs", 3, 1 + Q), A.subtract)
        tt("xr" + n, ("uu", e + 16, e + 3 * L, 48), W["rs"], ("nc", 15, M + 8, 8), A.add)
        tt("xs" + n, ("uu", e + 32, e + 3 * L, 48), W["lift"], ("nc", 7, M, 8), A.subtract)

        for i in range(2):
            a, o = PAD + SLOTS * M * i, (PAD + SLOTS * M) * i + PAD
            scan("cs%d%d" % (r, i), ("pa", o - 1, o + SLOTS * M), ("fa", a - 1, a + SLOTS * M), ("fb", a - 1, a + SLOTS * M),
                 0.0, A.add, A.add)
            scan("df%d%d" % (r, i), ("gg", 16 + M * i, 16 + M * (i + 1)), ("pa", o - 1, o + SLOTS * M - 1, SLOTS),
                 ("pa", o + SLOTS - 1, o + SLOTS * M, SLOTS), 0.0, A.max, A.subtract)
        for i, (a, b) in enumerate(((16, L + 16), (0, L + 32))):
            to = ("tt", i * L, i * L + b - a)
            turn("TN"[i] + n, to, ("gg", a, b))
            scan("U%d%d" % (r, i), ("uu", 3 * to[1], 3 * to[2], 3), to, ("mh", 0, b - a), 0.0, A.add, A.mult)

        order = ("pt", NODES + have + L, NODES + have + 2 * L)
        scan("xy" + n, W["xy"], ("uu", 45, 45 + 3 * L, 16), ("uu", e, e + 3 * L, 16), LIFT, A.min, A.add)
        ts("rv" + n, W["rv"], ("xy", 2, 3 * K, 3), col_i, A.add, 16.0 * (2 * SLOTS - 1) - LIFT, A.add)
        scatter("ss" + n, order, W["rv"], W["nrow"])

        for b in range(4):
            mm("ml%d%d" % (r, b), LAY[b], side("v" if r else "w", b), came if r else qz)
            act("h%d%d" % (r, b), ("h", b, 4 * L, 4), bank(LAY[b]), F.Relu, scale=0.015625)
        quant("qh" + n, qh, W["h"])
        if r == 0:
            hand("go0", "arr0", came, qh)
            hand("gw", "arrw", side("v", 0, 512), side("w", 0, 512))
        for b in range(4):
            mm("md%d%d" % (r, b), LAY[b], side("e", b), qh if r else came)

        for b in range(4):
            if r + 1 < R:
                copy("d%d%d" % (r, b), "sv", plane("pool", b, have, have + L), bank(LAY[b]))
            tt("w%d%d" % (r, b), plane("vt", b, have, have + L), bank(LAY[b]), plane("at", b, 0, L), A.add)
        for i in range(2):
            a, e = i * M, (i + 1) * M
            scan("xx%d%d" % (r, i), ("xx", a, e), ("ax", a, e), ("pt", order[1] + a, order[1] + e), 0.0, A.add, A.max)
            ts("to%d%d" % (r, i), ("topu", (r + 1) * K + a // 16, (r + 1) * K + e // 16), ("xx", a + 15, e, 16), col_c, A.subtract)
        if r + 1 == R:
            dma("ol", "y", "dout", T.ol[:], T.pt[0:128:16, order[1]:order[2]], [], [order])

    for r in range(R):
        one_round(r)

    reading(R)
    for k in range(4):
        dma("os%d" % k, "ys", "dout", T.osc[4 * k:4 * k + 4, :], T.z3p[32 * k:32 * k + 4, :], [], [W["z3p"]])
    for i in range(2):
        half = ("ys", i * M, (i + 1) * M)
        dma("oc%d" % i, "ys", "dout", T.oc[:, 4 * M * i:4 * M * (i + 1)], u8(side("z3", i, M)[0]), [], [side("z3", i, M)[0]])
        mm("my%d" % i, i, qu, side("z3", i, M))
        copy("y%d" % i, ("vs", "sv")[i], half, bank(i, 0, M))
        dma("oy%d" % i, ("ys", "sy")[i], "dout", T.y[:, i * M:(i + 1) * M], ap(half), [], [half])

    for name in ORDER.split() or list(steps):
        name, _, q = name.partition(".")
        qs, call, outs, ins, sem = steps.pop(name)
        issue(q or qs[0], call, outs, ins, sem)
    assert not steps

    g.wait_ge(T.sem.sent, 2 * lanes * (R + 1))
    for sem in sorted(total):
        g.wait_ge(T.sem[sem], total[sem])
